import numpy as np, ml_dtypes
CORES = [5,29,101,125,133,157,229,253]
N = 8
import mx_ref
BF = ml_dtypes.bfloat16
def gentries(a):
    return np.ascontiguousarray(a.reshape(8, 16, -1).transpose(0, 2, 1)).reshape(8, -1)
def gtable(e):
    e = np.asarray(e); return np.ascontiguousarray(e.reshape(8, -1, 16).transpose(0, 2, 1)).reshape(128, -1).astype(np.int32)
def gcols(t, e):
    v = np.concatenate([t.reshape(8, 16, -1, 4), np.zeros((8, 16, 1, 4), BF)], axis=2)
    return np.ascontiguousarray(np.stack([v[g][:, e[g]] for g in range(8)])).reshape(128, -1)
def tile(rs):
    return np.stack(rs, axis=2).reshape(128, -1).astype(BF)
def pick(q, e):
    c = np.concatenate([q[0].reshape(128, -1, 4), np.zeros((128, 1, 4), np.uint8)], axis=1); s = np.concatenate([q[1], np.ones((16, 1), np.uint8)], axis=1)
    return (np.ascontiguousarray(c[:, e].reshape(128, -1)), np.ascontiguousarray(s[:, e]))
def join(*qs):
    return (np.concatenate([q[0] for q in qs], axis=1), np.concatenate([q[1] for q in qs], axis=1))
def put(q, e, v):
    c, s = q[0].reshape(128, -1, 4).copy(), q[1].copy(); c[:, e] = v[0].reshape(128, -1, 4); s[:, e] = v[1]
    return (c.reshape(128, -1), s)
def pk(c, s):
    return (np.ascontiguousarray(c), mx_ref.live(s))
def emit(q):
    return q[0], q[1]
def packed(v, rng):
    q = [mx_ref.quantize(np.ascontiguousarray(v[r])) for r in range(N)]
    return np.stack([a for a, b in q]), np.stack([mx_ref.plane(b, rng) for a, b in q])
def values_of_codes():
    e, c = np.zeros((128, 128, 4), np.float32), np.zeros((128, 2, 4), np.uint8)
    e[np.arange(128), np.arange(128), 0] = 1
    c[:127, :, 0] = np.arange(256).reshape(2, 128).T[:127]
    return mx_ref.matmul(mx_ref.quantize(e.reshape(128, 512).astype(BF)), (c.reshape(128, 8), np.full((16, 2), 127, np.uint8))).T.reshape(-1).astype(np.float64)
CODE_VALUE, SCALE_VALUE = values_of_codes(), 2.0 ** (np.arange(256) - 127.0)
def decode(q):
    return (CODE_VALUE[q[0]].reshape(16, 8, -1, 4) * SCALE_VALUE[q[1]][:, None, :, None] + 0.0).reshape(128, -1).astype(np.float32)
def f(rng, *shape):
    return mx_ref.flush((rng.standard_normal(shape, dtype=np.float32) * np.exp2(rng.integers(-2, 3, shape[:-1] + (1,)))).astype(BF))
def wide(rng, *shape, cols=0):
    v = rng.standard_normal(shape, dtype=np.float32) * np.exp2(rng.integers(-12, 13, shape)).astype(np.float32)
    if cols: v *= np.repeat(np.exp2(rng.integers(-cols, cols + 1, shape[:-2] + (1, shape[-1] // 4))) * (rng.random(shape[:-2] + (1, shape[-1] // 4)) > 0.0625), 4, axis=-1).astype(np.float32)
    return mx_ref.flush(v.astype(BF))
C, M, WIDTH = 320, 40, 8
ROUNDS = 3
def big(v):
    v = v.astype(np.float32)
    v[np.abs(v) < np.float32(2.0 ** -16)] = 0
    return v.astype(BF)
def numbers_of(rng):
    return {"x": np.array(f(rng, N, 128, 4 * C)), "u": np.array(f(rng, N, 128, 512)), "v": np.array(f(rng, N, 128, 512))}
def towers(rng):
    return np.stack([gtable(np.stack([rng.permutation(C) for g in range(8)])) for r in range(N)])
def layers(rng):
    w = f(rng, N, 128, 2048).astype(np.float32).reshape(N, 128, 512, 4)
    w[rng.random(w.shape) < 0.9375] = 0
    m = np.searchsorted(28.0 * 2.0 ** np.arange(-20.0, 30.0), np.sum(np.abs(w), axis=(1, 3), keepdims=True))
    return np.array(mx_ref.flush((w * (2.0 ** (20.0 - m)).astype(np.float32)).astype(BF))).astype(np.float32)
def mirror(k):
    w, i = np.zeros((N, 128, 4, 128, 4), np.float32), np.arange(128)
    for b in range(4): w[:, i, b, i, b] = 32 * k[:, None]
    return w.reshape(N, 128, 512, 4)
def weights(rng, w):
    c, s = packed(np.ascontiguousarray(w).reshape(N, 128, 2048).astype(BF), rng)
    return {"wc": c, "ws": s}
def setup_inputs(rng):
    return {**numbers_of(rng), "tw": towers(rng), **weights(rng, layers(rng))}
def setup_inputs_ties(rng):
    d = numbers_of(rng)
    x = d["x"].astype(np.float32).reshape(N, 8, 16, C, 4)
    x[:, :, :8] = 0
    x[:, :, 0, :, 0] = rng.integers(0, 4, (N, 8, C))
    n = (N, 8, 8, C, 4)
    a = (1 + (2 * rng.integers(0, 64, n) + 1) / 128) * np.exp2(rng.integers(-14, -7, n)) * rng.choice([-1.0, 1.0], n)
    a[:, :, 0, :, 0] = 1.96875
    x[:, :, 8:] = a * np.exp2(rng.integers(-2, 3, (N, 8, 1, 1, 1)))
    u = d["u"].reshape(N, 128, 128, 4)
    u[:, :, ::16] = 0
    o = rng.permutation(N)
    for r in range(N):
        for h in range(0, 128, 16): u[r, h, h, 0] = 0.0 if r == o[0] else -1.0 if r in (o[1], o[3]) else 1.0
    w = layers(rng)
    w.reshape(N, 128, 4, 8, 16, 4)[:, :, :, :, :8] = 0
    return {"x": x.reshape(N, 128, 4 * C).astype(BF), "u": u.reshape(N, 128, 512), "v": d["v"], "tw": towers(rng), **weights(rng, w)}
def setup_inputs_near(rng):
    d = numbers_of(rng)
    x = d["x"].astype(np.float32).reshape(N, 8, 16, C, 4)
    u = d["u"].reshape(N, 128, 128, 4)
    u[:, :, ::16] = 0
    x[:, :, 0] = 0
    x[:, :, 8:] = 0
    s = rng.integers(0, 16, (N, 8, C))
    o = rng.permutation(8) % 4
    turn = np.arange(N) % 2 == rng.integers(2)
    w = mirror(np.ones(N)).reshape(N, 128, 4, 128, 4)
    for g in range(8):
        h = 16 * g
        if o[g] < 3:
            k = 2.0 ** -30 if o[g] == 2 else 1.0
            x[:, g, 0, :, 0] = -1.0 if o[g] == 1 else 1.0
            x[:, g, 8] = ((s[:, g, :, None] >> np.arange(4)) & 1) * np.exp2(np.arange(4) - 23.0)
            x[:, g, 11, :, 0] = 2.0 ** -10
            u[:, h, h, 0] = k
            u[:, h + 8, h] = k
            u[:, h + 11, h, 0] = k
            if o[g] == 0:
                x[turn, g, 8] = 0
                u[turn, h + 8, h] = -4.0
        else:
            x[:, g, 9:11, :, 0] = (1 + rng.integers(0, 8, (N, 2, C)) / 8) * 2.0 ** -30
            x[:, g, 12, :, 0] = 2.0 ** -30
            u[:, h + 9, h, 0] = -2.0 ** -30
            u[:, h + 10, h, 0] = 1.125 * 2.0 ** -30
            x[turn, g, 9:11] = 0
            u[turn, h + 9, h, 0] = 2.0 ** -30
            u[turn, h + 10, h, 0] = -1.125 * 2.0 ** -30
            for i in (h + 9, h + 10): w[turn, i, :, i] *= np.float32(2.0 ** -9)
    far = rng.permutation(np.nonzero(o < 3)[0])[:4]
    for r in range(N):
        for g in far: x[r, g, 0, rng.integers(C), 0] = 2.0 ** 30 * rng.choice([-1.0, 1.0])
    return {"x": x.reshape(N, 128, 4 * C).astype(BF), "u": u.reshape(N, 128, 512), "v": d["v"], "tw": towers(rng), **weights(rng, w)}
def setup_inputs_huge(rng):
    d = numbers_of(rng)
    o = rng.permutation(N)
    c = rng.choice([-1.0, 1.0], N)
    x = (0.6 + 0.4 * rng.random((N, 128, C, 4))) * 2.0 ** 30 * c[:, None, None, None]
    x[o < N // 2] *= rng.choice([-1.0, 1.0], (N // 2, 1, C, 1))
    u = d["u"].astype(np.float32).reshape(N, 128, 128, 4)
    k = np.stack([rng.permutation(8) % 2 * 2.0 - 1.0 for r in range(N)])
    u[:, :, ::16] = 2.0 ** 30 * (1 - 0.1 * rng.random((N, 128, 8, 4))) * k[:, None, :, None]
    e = int(np.argmax(o))
    a = np.where(rng.random((128, C, 4)) < rng.random((1, C, 1)), 0.9375, 1.0)
    a[::8, :, 0] = 1.0
    x[e] = a * 2.0 ** 30 * c[e]
    u[e, :, ::16] = 2.0 ** 30 * k[e][None, :, None]
    return {"x": x.astype(np.float32).reshape(N, 128, 4 * C).astype(BF), "u": u.reshape(N, 128, 512).astype(BF), "v": d["v"], "tw": towers(rng), **weights(rng, mirror(c * np.roll(c, 1)))}
def setup_inputs_ends(rng):
    d = numbers_of(rng)
    s, k0 = rng.choice([-1.0, 1.0]), int(rng.integers(4))
    x = d["x"].astype(np.float32).reshape(N, 128, C, 4)
    u = d["u"].astype(np.float32).reshape(N, 128, 128, 4)
    w, m, p = layers(rng), mirror(np.ones(N)), []
    for r in range(N):
        k = (r + k0) % 4
        c = (rng.permutation(8) % 2 * 2.0 - 1.0)[None, :, None]
        e = np.stack([rng.permutation(C)] * 8)
        if k == 0:
            x[r], w[r], u[r, :, ::16] = s * 2.0 ** 30, 0.0, 2.0 ** 30 * c
            e[:] = np.arange(C)
        elif k == 1:
            x[r], w[r], u[r, :, ::16] = s * 2.0 ** -30, m[r], 2.0 ** -30 * c
            e[:] = np.arange(C)[::-1]
        elif k == 2:
            x[r] = 2.0 ** 30 * rng.choice([-1.0, 1.0], (1, C, 1))
            w[r] = 0.0625 * rng.choice([-1.0, 1.0], (1, 512, 1))
            u[r, :, ::16] = 2.0 ** 30 * c
        else:
            for g in range(8): e[g] = np.roll(np.arange(C), g)
        p.append(gtable(e))
    d["v"] = (np.where(d["v"] < 0, -1.0, 1.0) * np.where(rng.permutation(N) % 2, 2.0 ** -30, 2.0 ** 30)[:, None, None]).astype(np.float32).astype(BF)
    return {"x": x.reshape(N, 128, 4 * C).astype(BF), "u": u.reshape(N, 128, 512).astype(BF), "v": d["v"], "tw": np.stack(p), **weights(rng, w)}
def setup_inputs_spread(rng):
    d = setup_inputs(rng)
    d["x"] = big(wide(rng, N, 128, 4 * C, cols=4))
    return d
def check_inputs(d):
    b = []
    for k in ("x", "u", "v"):
        a = np.abs(d[k].astype(np.float32))
        if not (np.isfinite(a).all() and ((a == 0) | (a >= 2.0 ** -30) & (a <= 2.0 ** 30)).all()): b.append("a value of " + k)
    none, least, most = [emit(mx_ref.quantize(np.full((128, 16), k, np.float32).astype(BF)))[1][0, 0] for k in (0.0, 2.0 ** -30, 2.0 ** 30)]
    for r in range(N):
        if (np.sort(gentries(d["tw"][r]), axis=1) != np.arange(C)).any(): b.append("tw: a group's entries aren't a permutation")
        if ((d["wc"][r] == 0x7F) | (d["wc"][r] == 0xFF)).any(): b.append("wc: a code that is no number")
        s = mx_ref.live(d["ws"][r])
        if ((s != none) & ((s < least) | (s > most))).any(): b.append("ws: a scale out of range")
        elif not (np.sum(np.abs(decode(pk(d["wc"][r], d["ws"][r])).astype(np.float64)).reshape(128, 512, 4), axis=(0, 2)) <= 32).all(): b.append("W: the sizes of a column are beyond 32 together")
    return b
def reference(x, u, v, tw, wc, ws):
    qu = [mx_ref.quantize(u[r]) for r in range(N)]
    lay = [pk(wc[r], ws[r]) for r in range(N)]
    now = [x[r] for r in range(N)]
    base = [gentries(tw[r]).reshape(8, M, WIDTH) for r in range(N)]
    top = [gentries(tw[r]).reshape(8, M, WIDTH) for r in range(N)]
    up = np.zeros((N, 8, C), np.int64)
    for t in range(ROUNDS):
        h = WIDTH >> (t + 1)
        own, ends = [], []
        for r in range(N):
            q = mx_ref.quantize(now[r])
            s = mx_ref.matmul(qu[r], q)[::16] + np.float32(0.0)
            own.append(decode(q).astype(BF))
            score = np.take_along_axis(s, base[r].reshape(8, -1), axis=1).reshape(8, M, 2 * h)
            o = np.argsort(-score, axis=2, kind="stable")
            b, e = np.take_along_axis(base[r], o, axis=2), np.take_along_axis(top[r], o, axis=2)
            np.put_along_axis(up[r], e[:, :, :h].reshape(8, -1), np.roll(b[:, :, h:], 1, axis=1).reshape(8, -1), axis=1)
            base[r], top[r] = b[:, :, :h], np.roll(e[:, :, h:], 1, axis=1)
            np.put_along_axis(up[r], top[r].reshape(8, -1), np.stack([C + np.arange(M * h)] * 8), axis=1)
            a = gcols(own[r], top[r].reshape(8, -1)).astype(np.float32) + gcols(own[r], base[r].reshape(8, -1)).astype(np.float32)
            ends.append(mx_ref.quantize(np.ascontiguousarray((a * np.float32(0.5)).astype(BF))))
        for r in range(N):
            made = tile([mx_ref.matmul(pick(lay[r], np.arange(128 * b, 128 * b + 128)), ends[r - 1]) * np.float32(0.03125) for b in range(4)])
            near = gcols(np.concatenate([own[r], made], axis=1), up[r]).astype(np.float32)
            now[r] = ((own[r].astype(np.float32) + near) * np.float32(0.5)).astype(BF)
    y, op = np.zeros((N, 128, C), np.float32), np.zeros((N, 8, C), np.float32)
    oc, osc = np.zeros((N, 128, 4 * C), np.uint8), np.zeros((N, 16, C), np.uint8)
    for r in range(N):
        q = mx_ref.quantize(now[r])
        y[r] = mx_ref.matmul(mx_ref.quantize(v[r]), q)
        op[r] = up[r]
        oc[r], osc[r] = emit(q)
    return {"y": y, "op": op, "oc": oc, "osc": osc}

@@ -1,0 +1,538 @@
+import numpy as np
+from concourse.bass import DstId, RemoteDMATransfer
+from concourse.mybir import dt, AluOpType, ActivationFunctionType
+
+F32, BF, I32, U16, U8, Q8 = "float32", "bfloat16", "int32", "uint16", "uint8", "float8_e4m3fn_x4"
+P = 128
+NE = {1: 160, 2: 80, 3: 40}
+NQ = {1: 160, 2: 128, 3: 128}
+PW = {1: 480, 2: 400, 3: 320}
+HL = {1: 4, 2: 2, 3: 1}
+
+SCRATCH = {}
+ALIAS = {}
+
+
+def _sb(name, n, d):
+    SCRATCH[name] = ("sbuf", [P, n], d)
+
+
+for _n, _c, _d in (
+        ("xt0", 1280, BF), ("xt1", 1280, BF), ("xt2", 1280, BF), ("xt3", 2560, BF), ("ut", 512, BF), ("vt", 512, BF),
+        ("twi", 20, I32), ("bt1", 20, U16), ("wcod", 512, Q8), ("wsca", 512, U8),
+        ("qu", 128, Q8), ("qus", 128, U8), ("qu2", 128, Q8), ("qu2s", 128, U8), ("qv", 128, Q8), ("qvs", 128, U8),
+        ("qe", 512, Q8), ("qes", 512, U8), ("qz", 128, Q8), ("qzs", 128, U8), ("zt", 512, BF),
+        ("babs", 516, F32), ("bnd", 516, BF), ("pint", 1, I32), ("prow", 1, I32), ("pa", 4, I32), ("pf", 8, F32),
+        ("uoi", 8, I32), ("uof", 8, U16), ("iow", 516, F32), ("rc8", 640, BF), ("rc4", 80, BF), ("upw", 640, F32),
+        ("cc1", 640, BF), ("cs1", 640, BF), ("cc2", 80, BF), ("cs2", 80, BF),
+        ("tabs", 128, U16), ("tab3", 32, U16), ("rb3", 64, F32), ("ru1", 176, F32), ("rb2", 96, F32),
+        ("gg", 1920, BF), ("lg3", 256, BF), ("zt3", 192, BF), ("h3", 192, BF), ("z3", 192, BF), ("yo", 320, F32),
+        ("ug1", 4 * 176, BF), ("ug2", 4 * 96, BF), ("qx", 1280, Q8), ("qxs", 1280, U8)):
+    _sb(_n, _c, _d)
+_at = 0
+for _n, _c in (
+        ("t1", 320), ("t2", 224), ("t3", 160), ("t16", 320), ("m1", 320), ("m2", 224), ("m3", 160), ("m16", 320),
+        ("rs4", 40), ("rs8", 40), ("rs16", 320), ("cu1", 160), ("cu2", 80), ("cu3", 48), ("cp", 4),
+        ("gp1", 320), ("sp1", 320), ("pp1", 160), ("pp2", 40), ("px2", 40), ("pp3", 16), ("px3", 16),
+        ("gb1", 160), ("gt1", 176), ("sb1", 160), ("st1", 160), ("gb2", 96), ("gt2", 112), ("sb2", 96), ("st2", 96),
+        ("eq1", 160), ("eq2", 40), ("eq3", 16), ("ma1", 160), ("mb1", 80), ("mc1", 40), ("rt1", 20),
+        ("ma2", 40), ("mb2", 20), ("rt2", 10), ("mx2", 40), ("my2", 20), ("ry2", 10),
+        ("ma3", 16), ("rt3", 8), ("mx3", 16), ("ry3", 8), ("tlf", 4), ("ucp", 4), ("um", 960), ("us", 960),
+        ("gs1", 320), ("gs2", 160), ("gs3", 96), ("sc1", 320), ("sc2", 160), ("sc3", 96)):
+    ALIAS[_n] = ("fa", _at)
+    _at += (_c + 7) // 8 * 8
+_sb("fa", _at, F32)
+for _t in (1, 2, 3):
+    _sb("ss%d" % _t, 320, F32)
+    _sb("v%d" % _t, 4 * PW[_t], BF)
+    _sb("fc%d" % _t, 800, BF)
+    _sb("et%d" % _t, 4 * NQ[_t], BF)
+    _sb("ec%d" % _t, NQ[_t], Q8)
+    _sb("es%d" % _t, NQ[_t], U8)
+    _sb("rc_%d" % _t, NE[_t], Q8)
+    _sb("rs_%d" % _t, NE[_t], U8)
+    _sb("lc%d" % _t, NQ[_t], Q8)
+    _sb("ls%d" % _t, NQ[_t], U8)
+for _b in range(4):
+    SCRATCH["pf%d" % _b] = ("psum", [P, 512], F32)
+    SCRATCH["ph%d" % _b] = ("psum", [P, 512], F32)
+
+SEMAPHORES = ["kv", "ks", "kt", "kg", "lo", "hop1", "hop2", "hop3", "ar1", "ar2", "ar3",
+              "dtw", "du", "dxa", "dxb", "dw", "dv", "dz", "dout"]
+
+TB = {"ux1": 0, "lx1": 12, "uo1": 22, "up1": 32, "ux2": 52, "lx2": 60, "uo2": 66, "up2": 72, "tl2": 92, "bu2": 98,
+      "lx3": 104, "ux3": 108, "uo3": 112, "tl3": 116, "bu3": 120}
+
+
+def relays(T, topo, r):
+    s, d = T.cores[r], T.cores[(r + 1) % len(T.cores)]
+    c = [k for k in topo.cores_of(s) if k != s and T.rank_of(k) is None and topo.may_write(k, d)]
+    c.sort(key=lambda k: (topo.die(k) != topo.die(s), k))
+    return s, d, c[0], c[1]
+
+
+def bits(es):
+    return sum(1 << e for e in es)
+
+
+def hand_on(g, core, T, topo):
+    for r in range(len(T.cores)):
+        s, d, ka, kb = relays(T, topo, r)
+        if core not in (ka, kb):
+            continue
+        rid, pid = topo.addr(d, core)
+        es = topo.engines(core, d)
+        n_in = len(topo.engines(s, core)) // 2
+        for t in (1, 2, 3):
+            n = NE[t]
+            g.wait_ge(T.sem["hop%d" % t], n_in)
+            if core == ka:
+                o, i = T["lc%d" % t][:, 0:n].bitcast(dt.uint8), T["rc_%d" % t][:, 0:n].bitcast(dt.uint8)
+            else:
+                o, i = T["ls%d" % t][:, 0:n], T["rs_%d" % t][:, 0:n]
+            g.remote_dma(out_ap=o, in_ap=i, remote_sem=T.sem["ar%d" % t], local_sem=T.sem.lo, pid=pid, routing_id=rid, dma_engine_mask=bits(es))
+        g.wait_ge(T.sem.lo, 3 * len(es))
+
+
+def rank_program(g, core, T, topo):
+    rank = T.rank_of(core)
+    if rank is None:
+        hand_on(g, core, T, topo)
+        return
+    A, AF = AluOpType, ActivationFunctionType
+    ADD, MUL, EQ, GT, GE = A.add, A.mult, A.is_equal, A.is_gt, A.is_ge
+    eng = {"v": g.vector, "s": g.scalar, "t": g.tensor, "y": g.sync, "g": g}
+    cnt, known, clock = {}, {k: {} for k in eng}, {}
+    wr, rd = {}, {}
+
+    def w_(name, a, b, s=1):
+        n, o = ALIAS.get(name, (name, 0))
+        return (n, o + a, o + b, s)
+
+    def ap(v):
+        return T[v[0]][:, v[1]:v[2]:v[3]] if v[3] > 1 else T[v[0]][:, v[1]:v[2]]
+
+    def clash(x, y):
+        if x[1] >= y[2] or y[1] >= x[2]:
+            return False
+        return not (x[3] == y[3] and x[3] > 1 and (x[1] - y[1]) % x[3])
+
+    def need(q, ev):
+        s, n = ev
+        if known[q].get(s, 0) >= n:
+            return
+        eng[q].wait_ge(T.sem[s], n)
+        for k, m in clock.get(ev, {}).items():
+            known[q][k] = max(known[q].get(k, 0), m)
+        known[q][s] = max(known[q].get(s, 0), n)
+
+    def order(q, reads, writes):
+        evs = {}
+        for v in reads:
+            psum = SCRATCH[v[0]][0] == "psum"
+            for x, ev, p in wr.get(v[0], []):
+                if clash(v, x):
+                    evs[ev[0]] = max(evs.get(ev[0], 0), ev[1])
+            if psum:
+                for x, ev, p in rd.get(v[0], []):
+                    if p != q:
+                        evs[ev[0]] = max(evs.get(ev[0], 0), ev[1])
+        for v in writes:
+            psum = SCRATCH[v[0]][0] == "psum"
+            for x, ev, p in wr.get(v[0], []):
+                if psum or clash(v, x):
+                    evs[ev[0]] = max(evs.get(ev[0], 0), ev[1])
+            for x, ev, p in rd.get(v[0], []):
+                if (psum or clash(v, x)) and p != q:
+                    evs[ev[0]] = max(evs.get(ev[0], 0), ev[1])
+        for s in sorted(evs):
+            need(q, (s, evs[s]))
+
+    def emit(q, call, reads, writes, sem=None, inc=1):
+        order(q, reads, writes)
+        sem = sem or "k" + q
+        cnt[sem] = cnt.get(sem, 0) + inc
+        ev = (sem, cnt[sem])
+        call().then_inc(T.sem[sem], inc)
+        c = dict(known[q])
+        c[sem] = cnt[sem]
+        clock[ev] = c
+        for v in writes:
+            wr.setdefault(v[0], []).append((v, ev, q))
+        for v in reads:
+            rd.setdefault(v[0], []).append((v, ev, q))
+
+    V, S, TE, G = g.vector, g.scalar, g.tensor, g
+
+    def fill(v, c):
+        emit("v", lambda: V.memset(ap(v), c), [], [v])
+
+    def tt(o, a, b, op, off=None):
+        if off is None:
+            emit("v", lambda: V.tensor_tensor(ap(o), ap(a), ap(b), op), [a, b], [o])
+        else:
+            emit("v", lambda: V.tensor_tensor(ap(o), ap(a).indirect(ap(off)), ap(b), op), [a, b, off], [o])
+
+    def ts(o, a, s1, op0, s2=None, op1=None):
+        r = [a] + ([s1] if isinstance(s1, tuple) else [])
+        s = ap(s1) if isinstance(s1, tuple) else s1
+        if op1 is None:
+            emit("v", lambda: V.tensor_scalar(ap(o), ap(a), s, None, op0), r, [o])
+        else:
+            emit("v", lambda: V.tensor_scalar(ap(o), ap(a), s, s2, op0, op1), r, [o])
+
+    def cp(o, a):
+        emit("v", lambda: V.tensor_copy(ap(o), ap(a)), [a], [o])
+
+    def put(o, off, a):
+        emit("v", lambda: V.tensor_copy(ap(o).indirect(ap(off)), ap(a)), [a, off], [o])
+
+    def scan(o, d0, d1):
+        emit("v", lambda: V.tensor_tensor_scan(ap(o), ap(d0), ap(d1), 0.0, MUL, ADD), [d0, d1], [o])
+
+    def quant(qo, so, i):
+        emit("v", lambda: V.quantize_mx(ap(qo), ap(so), ap(i)), [i], [qo, so])
+
+    def act(o, a, off=None, **kw):
+        i = (lambda: ap(a).indirect(ap(off))) if off is not None else (lambda: ap(a))
+        emit("s", lambda: S.activation(ap(o), i(), AF.Copy, **kw), [a] + ([off] if off is not None else []), [o])
+
+    def mm(o, l, ls, m, ms):
+        emit("t", lambda: TE.matmul_mx(ap(o), ap(l), ap(ls), ap(m), ap(ms), True, True), [l, ls, m, ms], [o])
+
+    def iota(v, pattern, base=0, cm=0):
+        if SCRATCH[v[0]][2] == I32:
+            emit("g", lambda: G.iota(ap(v), pattern, base, cm), [], [v])
+        else:
+            emit("g", lambda: G.iota(ap(v), pattern, base, cm, allow_small_or_imprecise_dtypes=True), [], [v])
+
+    def dma(q, o, i, reads, writes, sem):
+        emit(q, lambda: eng[q].dma_start(o, i), reads, writes, sem, 16)
+
+    def tab(name, k, j=0):
+        return w_("tabs", TB[name] + j, TB[name] + j + k)
+
+    def first_places():
+        tt(w_("gp1", 0, 320), w_("iow", 0, 320), w_("m1", 0, 320), MUL, w_("bt1", 0, 20))
+        yield 0
+        for k in range(8):
+            scan(w_("sp1", 40 * k, 40 * k + 40), w_("rs4", 0, 40), w_("gp1", k, 320, 8))
+            yield k
+        for l in range(2):
+            act(w_("pp1", l, 160, 2), w_("sp1", 3, 320, 4))
+        while True:
+            yield 8
+    gap = first_places()
+
+    dma("s", T.twi[:, :], T.tw[:, :], [], [w_("twi", 0, 20)], "dtw")
+    dma("y", T.xt0[:, 0:640], T.x[:, 0:640], [], [w_("xt0", 0, 640)], "dxa")
+    dma("s", T.ut[:, :], T.u[:, :], [], [w_("ut", 0, 512)], "du")
+    dma("y", T.xt0[:, 640:1280], T.x[:, 640:1280], [], [w_("xt0", 640, 1280)], "dxb")
+    dma("y", T.wcod[:, 0:512].bitcast(dt.uint8), T.wc[:, :], [], [w_("wcod", 0, 512)], "dw")
+    dma("y", T.wsca[:, 0:512], T.ws[:, :], [], [w_("wsca", 0, 512)], "dw")
+    for n in ("wcod", "wsca"):
+        wr[n] = [(w_(n, 0, 512), ("dw", 32), "y")]
+    dma("y", T.vt[:, :], T.v[:, :], [], [w_("vt", 0, 512)], "dv")
+
+    iota(w_("pint", 0, 1), [[1, 1]], 0, 1)
+    iota(w_("t1", 0, 320), [[0, 10], [1, 4], [0, 8]])
+    iota(w_("uoi", 0, 8), [[16, 8]])
+    iota(w_("iow", 0, 516), [[1, 516]])
+    iota(w_("t16", 0, 320), [[0, 20], [1, 16]])
+    iota(w_("t2", 0, 224), [[0, 7], [1, 8], [0, 4]])
+    iota(w_("t3", 0, 160), [[0, 5], [1, 16], [0, 2]])
+    iota(w_("cu1", 0, 156), [[1, 156]], 324)
+    iota(w_("cu1", 156, 160), [[1, 4]], 320)
+    iota(w_("cu2", 0, 78), [[1, 78]], 322)
+    iota(w_("cu2", 78, 80), [[1, 2]], 320)
+    iota(w_("cu3", 0, 39), [[1, 39]], 321)
+    iota(w_("cu3", 39, 48), [[1, 9]], 320)
+
+    fill(w_("rs4", 0, 40), 1.0)
+    fill(w_("cc1", 0, 640, 8), 0.0)
+    ts(w_("pf", 7, 8), w_("pint", 0, 1), -4.0, MUL, -3.0, ADD)
+    ts(w_("prow", 0, 1), w_("pint", 0, 1), 15, A.bitwise_and)
+    fill(w_("rc8", 0, 640), 1.0)
+    ts(w_("pa", 0, 1), w_("prow", 0, 1), 2, A.arith_shift_right)
+    ts(w_("pa", 1, 2), w_("prow", 0, 1), 1, A.arith_shift_right)
+    ts(w_("pa", 2, 3), w_("prow", 0, 1), 3, A.bitwise_and)
+    ts(w_("pa", 3, 4), w_("prow", 0, 1), 1, A.bitwise_and)
+    cp(w_("pf", 2, 3), w_("prow", 0, 1))
+    cp(w_("pf", 0, 2), w_("pa", 0, 2))
+    cp(w_("pf", 3, 5), w_("pa", 2, 4))
+    ts(w_("pf", 5, 6), w_("pa", 2, 3), 4.0, ADD)
+    ts(w_("pf", 6, 7), w_("pa", 3, 4), 2.0, ADD)
+    fill(w_("rs4", 0, 40, 4), 0.0)
+    fill(w_("rc8", 0, 640, 8), 0.0)
+    emit("s", lambda: S.activation(T.babs[:, 0:516], T.iow[:, 0:516], AF.Abs, bias=T.pf[:, 7:8]), [w_("iow", 0, 516), w_("pf", 7, 8)], [w_("babs", 0, 516)])
+    emit("s", lambda: S.activation(T.bnd[:, 0:516], T.babs[:, 0:516], AF.Relu, bias=0.5, scale=-0.5), [w_("babs", 0, 516)], [w_("bnd", 0, 516)])
+    ts(w_("m1", 0, 320), w_("t1", 0, 320), w_("pf", 0, 1), EQ)
+    fill(w_("eq3", 0, 16), 0.0)
+    fill(w_("pp3", 0, 16), 0.0)
+    fill(w_("px3", 0, 16), 0.0)
+    fill(w_("et2", 320, 512), 0.0)
+    fill(w_("et3", 192, 512), 0.0)
+    cp(w_("uof", 0, 8), w_("uoi", 0, 8))
+    cp(w_("bt1", 0, 20), w_("twi", 0, 20))
+    next(gap)
+    quant(w_("qu", 0, 128), w_("qus", 0, 128), w_("ut", 0, 512))
+    quant(w_("qx", 0, 160), w_("qxs", 0, 160), w_("xt0", 0, 640))
+    emit("v", lambda: V.tensor_copy(T.qu2[:, 0:128].bitcast(dt.uint32), T.qu[:, 0:128].bitcast(dt.uint32).indirect(T.uof[:, 0:8])),
+         [w_("qu", 0, 128), w_("uof", 0, 8)], [w_("qu2", 0, 128)])
+    act(w_("qu2s", 0, 128), w_("qus", 0, 128), w_("uof", 0, 8))
+
+    def late_constants():
+        fill(w_("zt", 0, 512), 0.0)
+        fill(w_("rs8", 0, 40), 1.0)
+        fill(w_("rc4", 0, 80), 1.0)
+        fill(w_("rs16", 0, 320), 1.0)
+        fill(w_("cc2", 0, 80, 4), 0.0)
+        fill(w_("upw", 0, 320), 0.0)
+        fill(w_("lg3", 0, 256), 0.0)
+        fill(w_("cp", 0, 2), 0.0)
+        fill(w_("rs8", 0, 40, 8), 0.0)
+        fill(w_("rc4", 0, 80, 4), 0.0)
+        fill(w_("rs16", 0, 320, 16), 0.0)
+        ts(w_("cp", 2, 3), w_("pf", 2, 3), 8.0, GE, 320.0, MUL)
+        ts(w_("m16", 0, 320), w_("t16", 0, 320), w_("pf", 2, 3), EQ)
+        ts(w_("m2", 0, 224), w_("t2", 0, 224), w_("pf", 1, 2), EQ)
+        ts(w_("m3", 0, 160), w_("t3", 0, 160), w_("pf", 2, 3), EQ)
+        quant(w_("qz", 0, 128), w_("qzs", 0, 128), w_("zt", 0, 512))
+        for t in (2, 3):
+            n = 128 - NE[t]
+            dma("y", T["lc%d" % t][:, NE[t]:128].bitcast(dt.uint8), T.qz[:, 0:n].bitcast(dt.uint8), [w_("qz", 0, n)], [w_("lc%d" % t, NE[t], 128)], "dz")
+            dma("y", T["ls%d" % t][:, NE[t]:128], T.qzs[:, 0:n], [w_("qzs", 0, n)], [w_("ls%d" % t, NE[t], 128)], "dz")
+        for t in (2, 3):
+            for n in ("lc%d" % t, "ls%d" % t):
+                wr[n] = [(w_(n, NE[t], 128), ("dz", 64), "y")]
+
+    s_, d_, ka, kb = relays(T, topo, rank)
+    lanes = [0]
+
+    def send(t):
+        n = NE[t]
+        for k, o, i, r in ((ka, T["rc_%d" % t][:, 0:n].bitcast(dt.uint8), T["ec%d" % t][:, 0:n].bitcast(dt.uint8), w_("ec%d" % t, 0, n)),
+                           (kb, T["rs_%d" % t][:, 0:n], T["es%d" % t][:, 0:n], w_("es%d" % t, 0, n))):
+            order("g", [r], [])
+            es = topo.engines(core, k)
+            half = es[:len(es) // 2] if k == ka else es[len(es) // 2:]
+            rid, pid = topo.addr(k, core)
+            g.remote_dma(out_ap=o, in_ap=i, remote_sem=T.sem["hop%d" % t], local_sem=T.sem.lo, pid=pid, routing_id=rid, dma_engine_mask=bits(half))
+            lanes[0] += len(half)
+
+    def place_list(t, out, clip):
+        u = 320 * (t - 1)
+        tt(w_("um", u, u + 320), w_("upw", 0, 320), w_("m16", 0, 320), MUL)
+        scan(w_("us", u, u + 320), w_("rs16", 0, 320), w_("um", u, u + 320))
+        if clip:
+            ts(out, w_("us", u + 15, u + 320, 16), 319.0, A.min)
+        else:
+            cp(out, w_("us", u + 15, u + 320, 16))
+
+    for t in (1, 2, 3):
+        h = HL[t]
+        w = 2 * h
+        ne, nq, pw = NE[t], NQ[t], PW[t]
+        qo = 320 * (t - 1)
+        x = "xt%d" % (t - 1)
+        for i in range(2):
+            if (t, i) != (1, 0):
+                quant(w_("qx", qo + 160 * i, qo + 160 * i + 160), w_("qxs", qo + 160 * i, qo + 160 * i + 160), w_(x, 640 * i, 640 * i + 640))
+            mm(w_("ph%d" % i, 0, 160), w_("qu2", 0, 128), w_("qu2s", 0, 128), w_("qx", qo + 160 * i, qo + 160 * i + 160), w_("qxs", qo + 160 * i, qo + 160 * i + 160))
+        if t == 1:
+            for b in range(4):
+                quant(w_("qe", 128 * b, 128 * b + 128), w_("qes", 128 * b, 128 * b + 128), w_("bnd", 3 - b, 515 - b))
+        for b in range(4):
+            mm(w_("pf%d" % b, 0, 320), w_("qe", 128 * b, 128 * b + 128), w_("qes", 128 * b, 128 * b + 128), w_("qx", qo, qo + 320), w_("qxs", qo, qo + 320))
+        ss, gs, sc, vn = "ss%d" % t, "gs%d" % t, "sc%d" % t, "v%d" % t
+        act(w_(ss, 0, 160), w_("ph0", 0, 160))
+        cp(w_(ss, 160, 320), w_("ph1", 0, 160))
+        for b in range(4):
+            act(w_(vn, pw * b, pw * b + 320), w_("pf%d" % b, 0, 320))
+        if t == 1:
+            next(gap)
+        ng = 40 * w if t < 3 else 96
+        bt = w_("bt1", 0, 20) if t == 1 else tab("lx%d" % (t - 1), ng // 16)
+        tt(w_(gs, 0, ng), w_(ss, 0, 320), w_("m%d" % t, 0, ng), MUL, bt)
+        if t == 1:
+            next(gap)
+        L = 40 if t < 3 else 48
+        T_ = 16 // h
+        rsn = {1: "rs4", 2: "rs8", 3: "rs16"}[t]
+        for k in range(w):
+            scan(w_(sc, L * k, L * k + L), w_(rsn, 0, L), w_(gs, k, ng, w))
+        if t == 1:
+            next(gap)
+        nc = L // T_
+        sv = lambda k0, k1: w_(sc, L * k0 + T_ - 1, L * k1, T_)
+        if t < 3:
+            cc, cs, eq, rt = "cc%d" % t, "cs%d" % t, "eq%d" % t, "rt%d" % t
+            for d in range(1, w):
+                above, below = w_(cc, d, w * nc * (w - d), w), w_(cc, w * nc * d + w - d, w * nc * w, w)
+                tt(above, sv(d, w), sv(0, w - d), GT)
+                if t == 1:
+                    act(below, above, scale=-1.0, bias=1.0)
+                else:
+                    tt(below, sv(0, w - d), sv(d, w), GE)
+            if t == 1:
+                next(gap)
+                next(gap)
+            scan(w_(cs, 0, w * w * nc), w_("rc8" if t == 1 else "rc4", 0, w * w * nc), w_(cc, 0, w * w * nc))
+            if t == 1:
+                next(gap)
+            n2 = 2 * w * nc
+            ts(w_(eq, 0, n2, 2), w_(cs, w - 1, w * w * nc, w), w_("pf", 2 + t, 3 + t), EQ)
+            ts(w_(eq, 1, n2, 2), w_(cs, w - 1, w * w * nc, w), w_("pf", 4 + t, 5 + t), EQ)
+            while t == 1 and next(gap) < 8:
+                pass
+
+            def pick(names, pay):
+                tt(w_(names[0], 0, n2), w_(eq, 0, n2), w_(pay, 0, n2), MUL)
+                n = n2 // 2
+                for a, o in zip(names, names[1:]):
+                    tt(w_(o, 0, n), w_(a, 0, n), w_(a, n, 2 * n), ADD)
+                    n //= 2
+            pick(("ma1", "mb1", "mc1", "rt1") if t == 1 else ("ma2", "mb2", "rt2"), "pp%d" % t)
+            nu = 16 + ne
+            cp(tab("ux%d" % t, nc, 1), w_(rt, 1, 2 * nc, 2))
+            cp(tab("ux%d" % t, 1), w_(rt, 2 * nc - 1, 2 * nc))
+            cp(tab("lx%d" % t, nc), w_(rt, 0, 2 * nc, 2))
+            ug = "ug%d" % t
+            for b in range(4):
+                act(w_(ug, nu * b, nu * b + nu), w_(vn, pw * b, pw * b + 320), tab("ux%d" % t, nu // 16))
+            for b in range(4):
+                tt(w_("et%d" % t, b, 4 * ne, 4), w_(vn, pw * b, pw * b + 320), w_(ug, nu * b + 16 - h, nu * b + 16 - h + ne), ADD, tab("lx%d" % t, ne // 16))
+        else:
+            for o, f in ((0, GE), (4, GT), (8, GT), (12, GE)):
+                a, b = (sv(0, 1), sv(1, 2)) if f == GE else (sv(1, 2), sv(0, 1))
+                tt(w_("eq3", o, o + 3), a, b, f)
+            tt(w_("ma3", 0, 16), w_("eq3", 0, 16), w_("pp3", 0, 16), MUL)
+            tt(w_("rt3", 0, 8), w_("ma3", 0, 8), w_("ma3", 8, 16), ADD)
+            cp(tab("lx3", 8), w_("rt3", 0, 8))
+            for b in range(4):
+                act(w_("lg3", 64 * b, 64 * b + 48), w_(vn, pw * b, pw * b + 320), tab("lx3", 3))
+            for b in range(4):
+                tt(w_("et3", b, 192, 4), w_(vn, pw * b, pw * b + 320), w_("lg3", 64 * b + 1, 64 * b + 49), ADD, tab("ux3", 3))
+        quant(w_("ec%d" % t, 0, nq), w_("es%d" % t, 0, nq), w_("et%d" % t, 0, 4 * nq))
+        send(t)
+
+        fc = "fc%d" % t
+
+        def second_copies():
+            for b in (0, 1):
+                act(w_(fc, 320 * b, 320 * b + 320), w_(vn, pw * b, pw * b + 320))
+            if t < 3:
+                act(w_(fc, 640, 800), w_(vn, pw * 3 + 160, pw * 3 + 320))
+
+        if t == 1:
+            act(w_("ru1", 0, 176), w_("iow", 0, 320), tab("ux1", 11))
+            second_copies()
+            late_constants()
+            cp(tab("uo1", 10), w_("rt1", 1, 20, 2))
+            put(w_("upw", 0, 640), tab("uo1", 10), w_("cu1", 0, 160))
+            put(w_("upw", 0, 640), tab("lx1", 10), w_("ru1", 12, 172))
+            place_list(1, tab("up1", 20), False)
+            tt(w_("gb1", 0, 160), w_("iow", 0, 320), w_("m2", 0, 160), MUL, tab("lx1", 10))
+            tt(w_("gt1", 0, 176), w_("iow", 0, 320), w_("m2", 20, 196), MUL, tab("ux1", 11))
+            for k in range(4):
+                scan(w_("sb1", 40 * k, 40 * k + 40), w_("rs8", 0, 40), w_("gb1", k, 160, 4))
+                scan(w_("st1", 40 * k, 40 * k + 40), w_("rs8", 0, 40), w_("gt1", 12 + k, 172, 4))
+            act(w_("pp2", 0, 40, 2), w_("sb1", 7, 160, 8))
+            act(w_("pp2", 1, 40, 2), w_("st1", 7, 160, 8))
+            act(w_("px2", 0, 40, 2), w_("st1", 7, 160, 8))
+            act(w_("px2", 1, 40, 2), w_("sb1", 7, 160, 8))
+        elif t == 2:
+            pick(("mx2", "my2", "ry2"), "px2")
+            cp(tab("bu2", 5, 1), w_("ry2", 1, 10, 2))
+            cp(tab("bu2", 1), w_("ry2", 9, 10))
+            act(w_("rb2", 0, 96), w_("iow", 0, 320), tab("bu2", 6))
+            second_copies()
+            cp(tab("tl2", 5), w_("ry2", 0, 10, 2))
+            cp(tab("uo2", 5), w_("rt2", 1, 10, 2))
+            put(w_("upw", 0, 640), tab("uo2", 5), w_("cu2", 0, 80))
+            put(w_("upw", 0, 640), tab("tl2", 5), w_("rb2", 14, 94))
+            place_list(2, tab("up2", 20), False)
+            cp(tab("lx2", 1, 5), w_("rt2", 0, 1))
+            cp(tab("ux2", 1, 6), w_("rt2", 1, 2))
+            tt(w_("gb2", 0, 96), w_("iow", 0, 320), w_("m3", 0, 96), MUL, tab("lx2", 6))
+            tt(w_("gt2", 0, 112), w_("iow", 0, 320), w_("m3", 18, 130), MUL, tab("ux2", 7))
+            for k in range(2):
+                scan(w_("sb2", 48 * k, 48 * k + 48), w_("rs16", 0, 48), w_("gb2", k, 96, 2))
+                scan(w_("st2", 48 * k, 48 * k + 48), w_("rs16", 0, 48), w_("gt2", 14 + k, 110, 2))
+            for k in range(2):
+                for o, s in ((0, "sb2"), (4, "st2")):
+                    act(w_("pp3", 8 * k + o, 8 * k + o + 3), w_(s, 48 * k + 15, 48 * k + 48, 16))
+                    act(w_("px3", 8 * k + 4 - o, 8 * k + 7 - o), w_(s, 48 * k + 15, 48 * k + 48, 16))
+        else:
+            tt(w_("mx3", 0, 16), w_("eq3", 0, 16), w_("px3", 0, 16), MUL)
+            tt(w_("ry3", 0, 8), w_("mx3", 0, 8), w_("mx3", 8, 16), ADD)
+            cp(tab("bu3", 3), w_("ry3", 4, 7))
+            act(w_("rb3", 1, 49), w_("iow", 0, 320), tab("bu3", 3))
+            act(w_("rb3", 0, 1), w_("rb3", 40, 41))
+            second_copies()
+            tt(w_("tlf", 0, 3), w_("ry3", 0, 3), w_("cp", 0, 3), ADD)
+            tt(w_("ucp", 0, 3), w_("rt3", 4, 7), w_("cp", 0, 3), ADD)
+            cp(tab("tl3", 3), w_("tlf", 0, 3))
+            for b in range(4):
+                ts(w_("tab3", 20 + 3 * b, 23 + 3 * b), w_("ucp", 0, 3), 4.0, MUL, float(b), ADD)
+            cp(tab("uo3", 3), w_("ucp", 0, 3))
+            put(w_("upw", 0, 640), tab("tl3", 3), w_("rb3", 0, 48))
+            place_list(3, w_("tab3", 0, 20), True)
+            for b in range(4):
+                act(w_("zt3", 48 * b, 48 * b + 48), w_(vn, pw * b, pw * b + 320), tab("ux3", 3))
+            for b in (2, 3):
+                act(w_("gg", 1280 + 320 * (b - 2), 1280 + 320 * (b - 1)), w_(vn, pw * b, pw * b + 320), w_("tab3", 0, 20))
+            for b in (0, 1):
+                tt(w_("xt3", b, 1280, 4), w_(vn, pw * b, pw * b + 320), w_(fc, 320 * b, 320 * b + 320), ADD, w_("tab3", 0, 20))
+            for b in (2, 3):
+                tt(w_("xt3", b, 1280, 4), w_("gg", 1280 + 320 * (b - 2), 1280 + 320 * (b - 1)), w_("pf%d" % b, 0, 320), ADD)
+            put(w_("upw", 0, 640), tab("uo3", 3), w_("cu3", 0, 48))
+            dma("y", T.op[:, :], T.upw[0:128:16, 0:320], [w_("upw", 0, 320)], [], "dout")
+        if t == 2:
+            quant(w_("qv", 0, 128), w_("qvs", 0, 128), w_("vt", 0, 512))
+
+        for n in ("lc%d" % t, "ls%d" % t):
+            wr.setdefault(n, []).append((w_(n, 0, ne), ("ar%d" % t, 2 * len(topo.engines(ka, d_))), "r"))
+        for b in ((0, 2, 1, 3) if t < 3 else (0, 1, 2, 3)):
+            mm(w_("ph%d" % b, 0, nq), w_("wcod", 128 * b, 128 * b + 128), w_("wsca", 128 * b, 128 * b + 128), w_("lc%d" % t, 0, nq), w_("ls%d" % t, 0, nq))
+        half = 0.015625
+        if t < 3:
+            gq = 640 * (t - 1)
+            win = lambda b: w_(vn, pw * b, pw * b + pw)
+            hv = lambda b: w_(vn, pw * b + 320, pw * b + 320 + ne)
+            ob, up = "xt%d" % t, "up%d" % t
+            act(hv(2), w_("ph2", 0, ne), scale=half)
+            act(hv(1), w_("ph1", 0, ne), scale=half)
+            act(w_("gg", gq, gq + 320), win(2), tab(up, 20))
+            act(hv(3), w_("ph3", 0, ne), scale=half)
+            act(w_("gg", gq + 320, gq + 480), win(3), tab(up, 10))
+            ts(hv(0), w_("ph0", 0, ne), half, MUL)
+            for b in (0, 1):
+                tt(w_(ob, b, 1280, 4), win(b), w_(fc, 320 * b, 320 * b + 320), ADD, tab(up, 20))
+            tt(w_(ob, 640 + 3, 1280, 4), win(3), w_(fc, 640, 800), ADD, tab(up, 10, 10))
+            tt(w_(ob, 2, 1280, 4), w_("gg", gq, gq + 320), w_("pf2", 0, 320), ADD)
+            tt(w_(ob, 3, 640, 4), w_("gg", gq + 320, gq + 480), w_("pf3", 0, 160), ADD)
+        else:
+            for b in range(4):
+                act(w_("h3", 48 * b, 48 * b + 48), w_("ph%d" % b, 0, 48), scale=half)
+            for b in range(4):
+                tt(w_("z3", 48 * b, 48 * b + 48), w_("zt3", 48 * b, 48 * b + 48), w_("h3", 48 * b, 48 * b + 48), ADD)
+                if b % 2:
+                    put(w_("xt3", 0, 2560), w_("tab3", 14 + 6 * (b // 2 + 1), 20 + 6 * (b // 2 + 1)), w_("z3", 96 * (b // 2), 96 * (b // 2) + 96))
+
+    for i in range(2):
+        a = 960 + 160 * i
+        quant(w_("qx", a, a + 160), w_("qxs", a, a + 160), w_("xt3", 640 * i, 640 * i + 640))
+        mm(w_("ph%d" % i, 0, 160), w_("qv", 0, 128), w_("qvs", 0, 128), w_("qx", a, a + 160), w_("qxs", a, a + 160))
+    dma("y", T.oc[:, :], T.qx[:, 960:1280].bitcast(dt.uint8), [w_("qx", 960, 1280)], [], "dout")
+    for k in range(4):
+        dma("y", T.osc[4 * k:4 * k + 4, 0:320], T.qxs[32 * k:32 * k + 4, 960:1280], [w_("qxs", 960, 1280)], [], "dout")
+    act(w_("yo", 0, 160), w_("ph0", 0, 160))
+    cp(w_("yo", 160, 320), w_("ph1", 0, 160))
+    dma("s", T.y[:, 0:160], T.yo[:, 0:160], [w_("yo", 0, 160)], [], "dout")
+    dma("y", T.y[:, 160:320], T.yo[:, 160:320], [w_("yo", 160, 320)], [], "dout")
+    g.wait_ge(T.sem.lo, lanes[0])
+    for s in sorted(cnt):
+        g.wait_ge(T.sem[s], cnt[s])
+    for t in (1, 2, 3):
+        g.wait_ge(T.sem["ar%d" % t], 2 * len(topo.engines(ka, d_)))

@@ -8,6 +8,9 @@ NE = {1: 160, 2: 80, 3: 40}
 NQ = {1: 160, 2: 128, 3: 128}
 PW = {1: 480, 2: 400, 3: 320}
 HL = {1: 4, 2: 2, 3: 1}
+NZ = 88
+LAND = {0: ("2", 40, NZ), 1: ("1", 0, 160), 2: ("2", 128, 80), 3: ("2", 0, 40)}
+READ = {1: ("1", 0), 2: ("2", 80), 3: ("2", 0)}
 
 SCRATCH = {}
 ALIAS = {}
@@ -22,16 +25,18 @@ for _n, _c, _d in (
         ("twi", 20, I32), ("bt1", 20, U16), ("wcod", 512, Q8), ("wsca", 512, U8),
         ("qu", 128, Q8), ("qus", 128, U8), ("qu2", 128, Q8), ("qu2s", 128, U8), ("qv", 128, Q8), ("qvs", 128, U8),
         ("qe", 512, Q8), ("qes", 512, U8), ("qz", 128, Q8), ("qzs", 128, U8), ("zt", 512, BF),
-        ("babs", 516, F32), ("bnd", 516, BF), ("pint", 1, I32), ("prow", 1, I32), ("pa", 4, I32), ("pf", 8, F32),
+        ("babs", 516, F32), ("bnd", 516, BF), ("pint", 1, I32), ("prow", 1, I32), ("pa", 4, I32), ("pf", 10, F32),
         ("uoi", 8, I32), ("uof", 8, U16), ("iow", 516, F32), ("rc8", 640, BF), ("rc4", 80, BF), ("upw", 640, F32),
         ("cc1", 640, BF), ("cs1", 640, BF), ("cc2", 80, BF), ("cs2", 80, BF),
         ("tabs", 128, U16), ("tab3", 32, U16), ("rb3", 64, F32), ("ru1", 176, F32), ("rb2", 96, F32),
         ("gg", 1920, BF), ("lg3", 256, BF), ("zt3", 192, BF), ("h3", 192, BF), ("z3", 192, BF), ("yo", 320, F32),
-        ("ug1", 4 * 176, BF), ("ug2", 4 * 96, BF), ("qx", 1280, Q8), ("qxs", 1280, U8)):
+        ("ug1", 4 * 176, BF), ("ug2", 4 * 96, BF), ("qx", 1280, Q8), ("qxs", 1280, U8),
+        ("rc_0", NZ, Q8), ("rs_0", NZ, U8), ("lc1", 160, Q8), ("ls1", 160, U8), ("lc2", 208, Q8), ("ls2", 208, U8)):
     _sb(_n, _c, _d)
 _at = 0
 for _n, _c in (
         ("t1", 320), ("t2", 224), ("t3", 160), ("t16", 320), ("m1", 320), ("m2", 224), ("m3", 160), ("m16", 320),
+        ("dm2", 224), ("dm3", 160), ("dm16", 320), ("ones", 320),
         ("rs4", 40), ("rs8", 40), ("rs16", 320), ("cu1", 160), ("cu2", 80), ("cu3", 48), ("cp", 4),
         ("gp1", 320), ("sp1", 320), ("pp1", 160), ("pp2", 40), ("px2", 40), ("pp3", 16), ("px3", 16),
         ("gb1", 160), ("gt1", 176), ("sb1", 160), ("st1", 160), ("gb2", 96), ("gt2", 112), ("sb2", 96), ("st2", 96),
@@ -51,14 +56,12 @@ for _t in (1, 2, 3):
     _sb("es%d" % _t, NQ[_t], U8)
     _sb("rc_%d" % _t, NE[_t], Q8)
     _sb("rs_%d" % _t, NE[_t], U8)
-    _sb("lc%d" % _t, NQ[_t], Q8)
-    _sb("ls%d" % _t, NQ[_t], U8)
 for _b in range(4):
     SCRATCH["pf%d" % _b] = ("psum", [P, 512], F32)
     SCRATCH["ph%d" % _b] = ("psum", [P, 512], F32)
 
-SEMAPHORES = ["kv", "ks", "kt", "kg", "lo", "hop1", "hop2", "hop3", "ar1", "ar2", "ar3",
-              "dtw", "du", "dxa", "dxb", "dw", "dv", "dz", "dout"]
+SEMAPHORES = ["kv", "ks", "kt", "kg", "lo", "hop0", "hop1", "hop2", "hop3", "ar0", "ar1", "ar2", "ar3",
+              "dtw", "du", "dxa", "dxb", "dw", "dv", "dout"]
 
 TB = {"ux1": 0, "lx1": 12, "uo1": 22, "up1": 32, "ux2": 52, "lx2": 60, "uo2": 66, "up2": 72, "tl2": 92, "bu2": 98,
       "lx3": 104, "ux3": 108, "uo3": 112, "tl3": 116, "bu3": 120}
@@ -83,15 +86,15 @@ def hand_on(g, core, T, topo):
         rid, pid = topo.addr(d, core)
         es = topo.engines(core, d)
         n_in = len(topo.engines(s, core)) // 2
-        for t in (1, 2, 3):
-            n = NE[t]
+        for t in (0, 1, 2, 3):
+            b, a, n = LAND[t]
             g.wait_ge(T.sem["hop%d" % t], n_in)
             if core == ka:
-                o, i = T["lc%d" % t][:, 0:n].bitcast(dt.uint8), T["rc_%d" % t][:, 0:n].bitcast(dt.uint8)
+                o, i = T["lc" + b][:, a:a + n].bitcast(dt.uint8), T["rc_%d" % t][:, 0:n].bitcast(dt.uint8)
             else:
-                o, i = T["ls%d" % t][:, 0:n], T["rs_%d" % t][:, 0:n]
+                o, i = T["ls" + b][:, a:a + n], T["rs_%d" % t][:, 0:n]
             g.remote_dma(out_ap=o, in_ap=i, remote_sem=T.sem["ar%d" % t], local_sem=T.sem.lo, pid=pid, routing_id=rid, dma_engine_mask=bits(es))
-        g.wait_ge(T.sem.lo, 3 * len(es))
+        g.wait_ge(T.sem.lo, 4 * len(es))
 
 
 def rank_program(g, core, T, topo):
@@ -224,20 +227,43 @@ def rank_program(g, core, T, topo):
             yield 8
     gap = first_places()
 
+    s_, d_, ka, kb = relays(T, topo, rank)
+    lanes = [0]
+
+    def send(t):
+        n = LAND[t][2]
+        c, s = ("ec%d" % t, "es%d" % t) if t else ("qz", "qzs")
+        for k, o, i, r in ((ka, T["rc_%d" % t][:, 0:n].bitcast(dt.uint8), T[c][:, 0:n].bitcast(dt.uint8), w_(c, 0, n)),
+                           (kb, T["rs_%d" % t][:, 0:n], T[s][:, 0:n], w_(s, 0, n))):
+            order("g", [r], [])
+            es = topo.engines(core, k)
+            half = es[:len(es) // 2] if k == ka else es[len(es) // 2:]
+            rid, pid = topo.addr(k, core)
+            g.remote_dma(out_ap=o, in_ap=i, remote_sem=T.sem["hop%d" % t], local_sem=T.sem.lo, pid=pid, routing_id=rid, dma_engine_mask=bits(half))
+            lanes[0] += len(half)
+
     dma("s", T.twi[:, :], T.tw[:, :], [], [w_("twi", 0, 20)], "dtw")
     dma("y", T.xt0[:, 0:640], T.x[:, 0:640], [], [w_("xt0", 0, 640)], "dxa")
     dma("s", T.ut[:, :], T.u[:, :], [], [w_("ut", 0, 512)], "du")
     dma("y", T.xt0[:, 640:1280], T.x[:, 640:1280], [], [w_("xt0", 640, 1280)], "dxb")
+    need("y", ("dxb", 16))
     dma("y", T.wcod[:, 0:512].bitcast(dt.uint8), T.wc[:, :], [], [w_("wcod", 0, 512)], "dw")
     dma("y", T.wsca[:, 0:512], T.ws[:, :], [], [w_("wsca", 0, 512)], "dw")
     for n in ("wcod", "wsca"):
         wr[n] = [(w_(n, 0, 512), ("dw", 32), "y")]
     dma("y", T.vt[:, :], T.v[:, :], [], [w_("vt", 0, 512)], "dv")
 
+    fill(w_("zt", 0, 512), 0.0)
+    fill(w_("ones", 0, 320), 1.0)
+    quant(w_("qz", 0, 128), w_("qzs", 0, 128), w_("zt", 0, 512))
     iota(w_("pint", 0, 1), [[1, 1]], 0, 1)
     iota(w_("t1", 0, 320), [[0, 10], [1, 4], [0, 8]])
     iota(w_("uoi", 0, 8), [[16, 8]])
     iota(w_("iow", 0, 516), [[1, 516]])
+    send(0)
+    for n, m, k in (("rs8", 40, 8), ("rs16", 320, 16), ("rc4", 80, 4)):
+        o, i = w_(n, 0, m), w_("ones", 0, m)
+        emit("g", lambda: G.affine_select(ap(o), ap(i), [[0, m // k], [1, k]], GT, 0.0, 0, 0), [i], [o])
     iota(w_("t16", 0, 320), [[0, 20], [1, 16]])
     iota(w_("t2", 0, 224), [[0, 7], [1, 8], [0, 4]])
     iota(w_("t3", 0, 160), [[0, 5], [1, 16], [0, 2]])
@@ -262,11 +288,17 @@ def rank_program(g, core, T, topo):
     cp(w_("pf", 3, 5), w_("pa", 2, 4))
     ts(w_("pf", 5, 6), w_("pa", 2, 3), 4.0, ADD)
     ts(w_("pf", 6, 7), w_("pa", 3, 4), 2.0, ADD)
+    ts(w_("pf", 8, 9), w_("pa", 1, 2), -1.0, MUL)
+    ts(w_("pf", 9, 10), w_("prow", 0, 1), -1.0, MUL)
     fill(w_("rs4", 0, 40, 4), 0.0)
     fill(w_("rc8", 0, 640, 8), 0.0)
     emit("s", lambda: S.activation(T.babs[:, 0:516], T.iow[:, 0:516], AF.Abs, bias=T.pf[:, 7:8]), [w_("iow", 0, 516), w_("pf", 7, 8)], [w_("babs", 0, 516)])
     emit("s", lambda: S.activation(T.bnd[:, 0:516], T.babs[:, 0:516], AF.Relu, bias=0.5, scale=-0.5), [w_("babs", 0, 516)], [w_("bnd", 0, 516)])
     ts(w_("m1", 0, 320), w_("t1", 0, 320), w_("pf", 0, 1), EQ)
+    fill(w_("lg3", 48, 256, 64), 0.0)
+    fill(w_("cp", 0, 2), 0.0)
+    fill(w_("cc2", 0, 80, 4), 0.0)
+    ts(w_("cp", 2, 3), w_("pf", 2, 3), 8.0, GE, 320.0, MUL)
     fill(w_("eq3", 0, 16), 0.0)
     fill(w_("pp3", 0, 16), 0.0)
     fill(w_("px3", 0, 16), 0.0)
@@ -281,44 +313,11 @@ def rank_program(g, core, T, topo):
          [w_("qu", 0, 128), w_("uof", 0, 8)], [w_("qu2", 0, 128)])
     act(w_("qu2s", 0, 128), w_("qus", 0, 128), w_("uof", 0, 8))
 
-    def late_constants():
-        fill(w_("zt", 0, 512), 0.0)
-        fill(w_("rs8", 0, 40), 1.0)
-        fill(w_("rc4", 0, 80), 1.0)
-        fill(w_("rs16", 0, 320), 1.0)
-        fill(w_("cc2", 0, 80, 4), 0.0)
-        fill(w_("upw", 0, 320), 0.0)
-        fill(w_("lg3", 0, 256), 0.0)
-        fill(w_("cp", 0, 2), 0.0)
-        fill(w_("rs8", 0, 40, 8), 0.0)
-        fill(w_("rc4", 0, 80, 4), 0.0)
-        fill(w_("rs16", 0, 320, 16), 0.0)
-        ts(w_("cp", 2, 3), w_("pf", 2, 3), 8.0, GE, 320.0, MUL)
-        ts(w_("m16", 0, 320), w_("t16", 0, 320), w_("pf", 2, 3), EQ)
-        ts(w_("m2", 0, 224), w_("t2", 0, 224), w_("pf", 1, 2), EQ)
-        ts(w_("m3", 0, 160), w_("t3", 0, 160), w_("pf", 2, 3), EQ)
-        quant(w_("qz", 0, 128), w_("qzs", 0, 128), w_("zt", 0, 512))
-        for t in (2, 3):
-            n = 128 - NE[t]
-            dma("y", T["lc%d" % t][:, NE[t]:128].bitcast(dt.uint8), T.qz[:, 0:n].bitcast(dt.uint8), [w_("qz", 0, n)], [w_("lc%d" % t, NE[t], 128)], "dz")
-            dma("y", T["ls%d" % t][:, NE[t]:128], T.qzs[:, 0:n], [w_("qzs", 0, n)], [w_("ls%d" % t, NE[t], 128)], "dz")
-        for t in (2, 3):
-            for n in ("lc%d" % t, "ls%d" % t):
-                wr[n] = [(w_(n, NE[t], 128), ("dz", 64), "y")]
-
-    s_, d_, ka, kb = relays(T, topo, rank)
-    lanes = [0]
-
-    def send(t):
-        n = NE[t]
-        for k, o, i, r in ((ka, T["rc_%d" % t][:, 0:n].bitcast(dt.uint8), T["ec%d" % t][:, 0:n].bitcast(dt.uint8), w_("ec%d" % t, 0, n)),
-                           (kb, T["rs_%d" % t][:, 0:n], T["es%d" % t][:, 0:n], w_("es%d" % t, 0, n))):
-            order("g", [r], [])
-            es = topo.engines(core, k)
-            half = es[:len(es) // 2] if k == ka else es[len(es) // 2:]
-            rid, pid = topo.addr(k, core)
-            g.remote_dma(out_ap=o, in_ap=i, remote_sem=T.sem["hop%d" % t], local_sem=T.sem.lo, pid=pid, routing_id=rid, dma_engine_mask=bits(half))
-            lanes[0] += len(half)
+    def late_masks():
+        for m, t, n, c in (("m16", "t16", 320, 9), ("m2", "t2", 224, 8), ("m3", "t3", 160, 9)):
+            i, o, d, b = w_(t, 0, n), w_(m, 0, n), w_("d" + m, 0, n), w_("pf", c, c + 1)
+            emit("s", lambda: S.activation(ap(d), ap(i), AF.Abs, bias=ap(b)), [i, b], [d])
+            emit("s", lambda: S.activation(ap(o), ap(d), AF.Relu, bias=1.0, scale=-1.0), [d], [o])
 
     def place_list(t, out, clip):
         u = 320 * (t - 1)
@@ -426,8 +425,8 @@ def rank_program(g, core, T, topo):
 
         if t == 1:
             act(w_("ru1", 0, 176), w_("iow", 0, 320), tab("ux1", 11))
+            late_masks()
             second_copies()
-            late_constants()
             cp(tab("uo1", 10), w_("rt1", 1, 20, 2))
             put(w_("upw", 0, 640), tab("uo1", 10), w_("cu1", 0, 160))
             put(w_("upw", 0, 640), tab("lx1", 10), w_("ru1", 12, 172))
@@ -486,27 +485,30 @@ def rank_program(g, core, T, topo):
                 tt(w_("xt3", b, 1280, 4), w_(vn, pw * b, pw * b + 320), w_(fc, 320 * b, 320 * b + 320), ADD, w_("tab3", 0, 20))
             for b in (2, 3):
                 tt(w_("xt3", b, 1280, 4), w_("gg", 1280 + 320 * (b - 2), 1280 + 320 * (b - 1)), w_("pf%d" % b, 0, 320), ADD)
-            put(w_("upw", 0, 640), tab("uo3", 3), w_("cu3", 0, 48))
-            dma("y", T.op[:, :], T.upw[0:128:16, 0:320], [w_("upw", 0, 320)], [], "dout")
         if t == 2:
             quant(w_("qv", 0, 128), w_("qvs", 0, 128), w_("vt", 0, 512))
 
-        for n in ("lc%d" % t, "ls%d" % t):
-            wr.setdefault(n, []).append((w_(n, 0, ne), ("ar%d" % t, 2 * len(topo.engines(ka, d_))), "r"))
+        for n in ("lc", "ls"):
+            for k in (t, 0):
+                b, a, m = LAND[k]
+                wr.setdefault(n + b, []).append((w_(n + b, a, a + m), ("ar%d" % k, 2 * len(topo.engines(ka, d_))), "r"))
+        rb, ra = READ[t]
+        hs = LAND[t][1] - ra
         for b in ((0, 2, 1, 3) if t < 3 else (0, 1, 2, 3)):
-            mm(w_("ph%d" % b, 0, nq), w_("wcod", 128 * b, 128 * b + 128), w_("wsca", 128 * b, 128 * b + 128), w_("lc%d" % t, 0, nq), w_("ls%d" % t, 0, nq))
+            mm(w_("ph%d" % b, 0, nq), w_("wcod", 128 * b, 128 * b + 128), w_("wsca", 128 * b, 128 * b + 128), w_("lc" + rb, ra, ra + nq), w_("ls" + rb, ra, ra + nq))
         half = 0.015625
         if t < 3:
             gq = 640 * (t - 1)
             win = lambda b: w_(vn, pw * b, pw * b + pw)
             hv = lambda b: w_(vn, pw * b + 320, pw * b + 320 + ne)
+            hp = lambda b: w_("ph%d" % b, hs, hs + ne)
             ob, up = "xt%d" % t, "up%d" % t
-            act(hv(2), w_("ph2", 0, ne), scale=half)
-            act(hv(1), w_("ph1", 0, ne), scale=half)
+            act(hv(2), hp(2), scale=half)
+            act(hv(1), hp(1), scale=half)
             act(w_("gg", gq, gq + 320), win(2), tab(up, 20))
-            act(hv(3), w_("ph3", 0, ne), scale=half)
+            act(hv(3), hp(3), scale=half)
             act(w_("gg", gq + 320, gq + 480), win(3), tab(up, 10))
-            ts(hv(0), w_("ph0", 0, ne), half, MUL)
+            ts(hv(0), hp(0), half, MUL)
             for b in (0, 1):
                 tt(w_(ob, b, 1280, 4), win(b), w_(fc, 320 * b, 320 * b + 320), ADD, tab(up, 20))
             tt(w_(ob, 640 + 3, 1280, 4), win(3), w_(fc, 640, 800), ADD, tab(up, 10, 10))
@@ -524,9 +526,11 @@ def rank_program(g, core, T, topo):
         a = 960 + 160 * i
         quant(w_("qx", a, a + 160), w_("qxs", a, a + 160), w_("xt3", 640 * i, 640 * i + 640))
         mm(w_("ph%d" % i, 0, 160), w_("qv", 0, 128), w_("qvs", 0, 128), w_("qx", a, a + 160), w_("qxs", a, a + 160))
+    put(w_("upw", 0, 640), tab("uo3", 3), w_("cu3", 0, 48))
     dma("y", T.oc[:, :], T.qx[:, 960:1280].bitcast(dt.uint8), [w_("qx", 960, 1280)], [], "dout")
     for k in range(4):
         dma("y", T.osc[4 * k:4 * k + 4, 0:320], T.qxs[32 * k:32 * k + 4, 960:1280], [w_("qxs", 960, 1280)], [], "dout")
+    dma("y", T.op[:, :], T.upw[0:128:16, 0:320], [w_("upw", 0, 320)], [], "dout")
     act(w_("yo", 0, 160), w_("ph0", 0, 160))
     cp(w_("yo", 160, 320), w_("ph1", 0, 160))
     dma("s", T.y[:, 0:160], T.yo[:, 0:160], [w_("yo", 0, 160)], [], "dout")
@@ -534,5 +538,5 @@ def rank_program(g, core, T, topo):
     g.wait_ge(T.sem.lo, lanes[0])
     for s in sorted(cnt):
         g.wait_ge(T.sem[s], cnt[s])
-    for t in (1, 2, 3):
+    for t in (0, 1, 2, 3):
         g.wait_ge(T.sem["ar%d" % t], 2 * len(topo.engines(ka, d_)))

@@ -25,7 +25,7 @@ for _n, _c, _d in (
         ("twi", 20, I32), ("bt1", 20, U16), ("wcod", 512, Q8), ("wsca", 512, U8),
         ("qu", 128, Q8), ("qus", 128, U8), ("qu2", 128, Q8), ("qu2s", 128, U8), ("qv", 128, Q8), ("qvs", 128, U8),
         ("qe", 512, Q8), ("qes", 512, U8), ("qz", 128, Q8), ("qzs", 128, U8), ("zt", 512, BF),
-        ("babs", 516, F32), ("bnd", 516, BF), ("pint", 1, I32), ("prow", 1, I32), ("pa", 4, I32), ("pf", 10, F32),
+        ("babs", 516, F32), ("bnd", 516, BF), ("pint", 1, I32), ("prow", 1, I32), ("pa", 4, I32), ("pf", 11, F32),
         ("uoi", 8, I32), ("uof", 8, U16), ("iow", 516, F32), ("rc8", 640, BF), ("rc4", 80, BF), ("upw", 640, F32),
         ("cc1", 640, BF), ("cs1", 640, BF), ("cc2", 80, BF), ("cs2", 80, BF),
         ("tabs", 128, U16), ("tab3", 32, U16), ("rb3", 64, F32), ("ru1", 176, F32), ("rb2", 96, F32),
@@ -36,13 +36,13 @@ for _n, _c, _d in (
 _at = 0
 for _n, _c in (
         ("t1", 320), ("t2", 224), ("t3", 160), ("t16", 320), ("m1", 320), ("m2", 224), ("m3", 160), ("m16", 320),
-        ("dm2", 224), ("dm3", 160), ("dm16", 320), ("ones", 320),
-        ("rs4", 40), ("rs8", 40), ("rs16", 320), ("cu1", 160), ("cu2", 80), ("cu3", 48), ("cp", 4),
+        ("dm2", 224), ("dm3", 160), ("dm16", 320), ("ones", 320), ("dp", 320),
+        ("rs4", 40), ("rs8", 40), ("rs16", 48), ("cu1", 160), ("cu2", 80), ("cu3", 48), ("cp", 4),
         ("gp1", 320), ("sp1", 320), ("pp1", 160), ("pp2", 40), ("px2", 40), ("pp3", 16), ("px3", 16),
         ("gb1", 160), ("gt1", 176), ("sb1", 160), ("st1", 160), ("gb2", 96), ("gt2", 112), ("sb2", 96), ("st2", 96),
         ("eq1", 160), ("eq2", 40), ("eq3", 16), ("ma1", 160), ("mb1", 80), ("mc1", 40), ("rt1", 20),
         ("ma2", 40), ("mb2", 20), ("rt2", 10), ("mx2", 40), ("my2", 20), ("ry2", 10),
-        ("ma3", 16), ("rt3", 8), ("mx3", 16), ("ry3", 8), ("tlf", 4), ("ucp", 4), ("um", 960), ("us", 960),
+        ("ma3", 16), ("rt3", 8), ("mx3", 16), ("ry3", 8), ("tlf", 4), ("ucp", 4), ("us", 960),
         ("gs1", 320), ("gs2", 160), ("gs3", 96), ("sc1", 320), ("sc2", 160), ("sc3", 96)):
     ALIAS[_n] = ("fa", _at)
     _at += (_c + 7) // 8 * 8
@@ -85,7 +85,7 @@ def hand_on(g, core, T, topo):
             continue
         rid, pid = topo.addr(d, core)
         es = topo.engines(core, d)
-        n_in = len(topo.engines(s, core)) // 2
+        n_in = len(topo.engines(s, core))
         for t in (0, 1, 2, 3):
             b, a, n = LAND[t]
             g.wait_ge(T.sem["hop%d" % t], n_in)
@@ -187,6 +187,9 @@ def rank_program(g, core, T, topo):
     def cp(o, a):
         emit("v", lambda: V.tensor_copy(ap(o), ap(a)), [a], [o])
 
+    def take(o, a, off):
+        emit("v", lambda: V.tensor_copy(ap(o), ap(a).indirect(ap(off))), [a, off], [o])
+
     def put(o, off, a):
         emit("v", lambda: V.tensor_copy(ap(o).indirect(ap(off)), ap(a)), [a, off], [o])
 
@@ -237,10 +240,9 @@ def rank_program(g, core, T, topo):
                            (kb, T["rs_%d" % t][:, 0:n], T[s][:, 0:n], w_(s, 0, n))):
             order("g", [r], [])
             es = topo.engines(core, k)
-            half = es[:len(es) // 2] if k == ka else es[len(es) // 2:]
             rid, pid = topo.addr(k, core)
-            g.remote_dma(out_ap=o, in_ap=i, remote_sem=T.sem["hop%d" % t], local_sem=T.sem.lo, pid=pid, routing_id=rid, dma_engine_mask=bits(half))
-            lanes[0] += len(half)
+            g.remote_dma(out_ap=o, in_ap=i, remote_sem=T.sem["hop%d" % t], local_sem=T.sem.lo, pid=pid, routing_id=rid, dma_engine_mask=bits(es))
+            lanes[0] += len(es)
 
     dma("s", T.twi[:, :], T.tw[:, :], [], [w_("twi", 0, 20)], "dtw")
     dma("y", T.xt0[:, 0:640], T.x[:, 0:640], [], [w_("xt0", 0, 640)], "dxa")
@@ -254,14 +256,14 @@ def rank_program(g, core, T, topo):
     dma("y", T.vt[:, :], T.v[:, :], [], [w_("vt", 0, 512)], "dv")
 
     fill(w_("zt", 0, 512), 0.0)
-    fill(w_("ones", 0, 320), 1.0)
+    fill(w_("ones", 0, 80), 1.0)
     quant(w_("qz", 0, 128), w_("qzs", 0, 128), w_("zt", 0, 512))
     iota(w_("pint", 0, 1), [[1, 1]], 0, 1)
     iota(w_("t1", 0, 320), [[0, 10], [1, 4], [0, 8]])
     iota(w_("uoi", 0, 8), [[16, 8]])
     iota(w_("iow", 0, 516), [[1, 516]])
     send(0)
-    for n, m, k in (("rs8", 40, 8), ("rs16", 320, 16), ("rc4", 80, 4)):
+    for n, m, k in (("rs8", 40, 8), ("rs16", 48, 16), ("rc4", 80, 4)):
         o, i = w_(n, 0, m), w_("ones", 0, m)
         emit("g", lambda: G.affine_select(ap(o), ap(i), [[0, m // k], [1, k]], GT, 0.0, 0, 0), [i], [o])
     iota(w_("t16", 0, 320), [[0, 20], [1, 16]])
@@ -288,22 +290,11 @@ def rank_program(g, core, T, topo):
     cp(w_("pf", 3, 5), w_("pa", 2, 4))
     ts(w_("pf", 5, 6), w_("pa", 2, 3), 4.0, ADD)
     ts(w_("pf", 6, 7), w_("pa", 3, 4), 2.0, ADD)
-    ts(w_("pf", 8, 9), w_("pa", 1, 2), -1.0, MUL)
-    ts(w_("pf", 9, 10), w_("prow", 0, 1), -1.0, MUL)
     fill(w_("rs4", 0, 40, 4), 0.0)
     fill(w_("rc8", 0, 640, 8), 0.0)
     emit("s", lambda: S.activation(T.babs[:, 0:516], T.iow[:, 0:516], AF.Abs, bias=T.pf[:, 7:8]), [w_("iow", 0, 516), w_("pf", 7, 8)], [w_("babs", 0, 516)])
     emit("s", lambda: S.activation(T.bnd[:, 0:516], T.babs[:, 0:516], AF.Relu, bias=0.5, scale=-0.5), [w_("babs", 0, 516)], [w_("bnd", 0, 516)])
     ts(w_("m1", 0, 320), w_("t1", 0, 320), w_("pf", 0, 1), EQ)
-    fill(w_("lg3", 48, 256, 64), 0.0)
-    fill(w_("cp", 0, 2), 0.0)
-    fill(w_("cc2", 0, 80, 4), 0.0)
-    ts(w_("cp", 2, 3), w_("pf", 2, 3), 8.0, GE, 320.0, MUL)
-    fill(w_("eq3", 0, 16), 0.0)
-    fill(w_("pp3", 0, 16), 0.0)
-    fill(w_("px3", 0, 16), 0.0)
-    fill(w_("et2", 320, 512), 0.0)
-    fill(w_("et3", 192, 512), 0.0)
     cp(w_("uof", 0, 8), w_("uoi", 0, 8))
     cp(w_("bt1", 0, 20), w_("twi", 0, 20))
     next(gap)
@@ -318,15 +309,17 @@ def rank_program(g, core, T, topo):
             i, o, d, b = w_(t, 0, n), w_(m, 0, n), w_("d" + m, 0, n), w_("pf", c, c + 1)
             emit("s", lambda: S.activation(ap(d), ap(i), AF.Abs, bias=ap(b)), [i, b], [d])
             emit("s", lambda: S.activation(ap(o), ap(d), AF.Relu, bias=1.0, scale=-1.0), [d], [o])
+            if m == "m16":
+                act(w_("dp", 0, 320), o, scale=-1000000.0, bias=1024.0)
 
     def place_list(t, out, clip):
         u = 320 * (t - 1)
-        tt(w_("um", u, u + 320), w_("upw", 0, 320), w_("m16", 0, 320), MUL)
-        scan(w_("us", u, u + 320), w_("rs16", 0, 320), w_("um", u, u + 320))
+        o, a, b, e = w_("us", u, u + 320), w_("dp", 0, 320), w_("upw", 0, 320), w_("us", u + 15, u + 320, 16)
+        emit("v", lambda: V.tensor_tensor_scan(ap(o), ap(a), ap(b), 0.0, ADD, A.max), [a, b], [o])
         if clip:
-            ts(out, w_("us", u + 15, u + 320, 16), 319.0, A.min)
+            ts(out, e, w_("pf", 10, 11), ADD, 319.0, A.min)
         else:
-            cp(out, w_("us", u + 15, u + 320, 16))
+            ts(out, e, w_("pf", 10, 11), ADD)
 
     for t in (1, 2, 3):
         h = HL[t]
@@ -339,14 +332,14 @@ def rank_program(g, core, T, topo):
                 quant(w_("qx", qo + 160 * i, qo + 160 * i + 160), w_("qxs", qo + 160 * i, qo + 160 * i + 160), w_(x, 640 * i, 640 * i + 640))
             mm(w_("ph%d" % i, 0, 160), w_("qu2", 0, 128), w_("qu2s", 0, 128), w_("qx", qo + 160 * i, qo + 160 * i + 160), w_("qxs", qo + 160 * i, qo + 160 * i + 160))
         if t == 1:
-            for b in range(4):
+            for b in (3, 0, 1, 2):
                 quant(w_("qe", 128 * b, 128 * b + 128), w_("qes", 128 * b, 128 * b + 128), w_("bnd", 3 - b, 515 - b))
-        for b in range(4):
+        for b in (3, 0, 1, 2):
             mm(w_("pf%d" % b, 0, 320), w_("qe", 128 * b, 128 * b + 128), w_("qes", 128 * b, 128 * b + 128), w_("qx", qo, qo + 320), w_("qxs", qo, qo + 320))
         ss, gs, sc, vn = "ss%d" % t, "gs%d" % t, "sc%d" % t, "v%d" % t
         act(w_(ss, 0, 160), w_("ph0", 0, 160))
         cp(w_(ss, 160, 320), w_("ph1", 0, 160))
-        for b in range(4):
+        for b in ((3, 0, 1, 2) if t > 1 else (3, 0)):
             act(w_(vn, pw * b, pw * b + 320), w_("pf%d" % b, 0, 320))
         if t == 1:
             next(gap)
@@ -355,12 +348,14 @@ def rank_program(g, core, T, topo):
         tt(w_(gs, 0, ng), w_(ss, 0, 320), w_("m%d" % t, 0, ng), MUL, bt)
         if t == 1:
             next(gap)
+            next(gap)
         L = 40 if t < 3 else 48
         T_ = 16 // h
         rsn = {1: "rs4", 2: "rs8", 3: "rs16"}[t]
         for k in range(w):
             scan(w_(sc, L * k, L * k + L), w_(rsn, 0, L), w_(gs, k, ng, w))
         if t == 1:
+            next(gap)
             next(gap)
         nc = L // T_
         sv = lambda k0, k1: w_(sc, L * k0 + T_ - 1, L * k1, T_)
@@ -374,16 +369,14 @@ def rank_program(g, core, T, topo):
                 else:
                     tt(below, sv(0, w - d), sv(d, w), GE)
             if t == 1:
-                next(gap)
-                next(gap)
+                while next(gap) < 8:
+                    pass
+                for b in (1, 2):
+                    act(w_(vn, pw * b, pw * b + 320), w_("pf%d" % b, 0, 320))
             scan(w_(cs, 0, w * w * nc), w_("rc8" if t == 1 else "rc4", 0, w * w * nc), w_(cc, 0, w * w * nc))
-            if t == 1:
-                next(gap)
             n2 = 2 * w * nc
             ts(w_(eq, 0, n2, 2), w_(cs, w - 1, w * w * nc, w), w_("pf", 2 + t, 3 + t), EQ)
             ts(w_(eq, 1, n2, 2), w_(cs, w - 1, w * w * nc, w), w_("pf", 4 + t, 5 + t), EQ)
-            while t == 1 and next(gap) < 8:
-                pass
 
             def pick(names, pay):
                 tt(w_(names[0], 0, n2), w_(eq, 0, n2), w_(pay, 0, n2), MUL)
@@ -397,9 +390,10 @@ def rank_program(g, core, T, topo):
             cp(tab("ux%d" % t, 1), w_(rt, 2 * nc - 1, 2 * nc))
             cp(tab("lx%d" % t, nc), w_(rt, 0, 2 * nc, 2))
             ug = "ug%d" % t
-            for b in range(4):
+            for b in (0, 1, 2):
                 act(w_(ug, nu * b, nu * b + nu), w_(vn, pw * b, pw * b + 320), tab("ux%d" % t, nu // 16))
-            for b in range(4):
+            take(w_(ug, nu * 3, nu * 4), w_(vn, pw * 3, pw * 3 + 320), tab("ux%d" % t, nu // 16))
+            for b in (3, 0, 1, 2):
                 tt(w_("et%d" % t, b, 4 * ne, 4), w_(vn, pw * b, pw * b + 320), w_(ug, nu * b + 16 - h, nu * b + 16 - h + ne), ADD, tab("lx%d" % t, ne // 16))
         else:
             for o, f in ((0, GE), (4, GT), (8, GT), (12, GE)):
@@ -408,9 +402,10 @@ def rank_program(g, core, T, topo):
             tt(w_("ma3", 0, 16), w_("eq3", 0, 16), w_("pp3", 0, 16), MUL)
             tt(w_("rt3", 0, 8), w_("ma3", 0, 8), w_("ma3", 8, 16), ADD)
             cp(tab("lx3", 8), w_("rt3", 0, 8))
-            for b in range(4):
+            for b in (0, 1, 2):
                 act(w_("lg3", 64 * b, 64 * b + 48), w_(vn, pw * b, pw * b + 320), tab("lx3", 3))
-            for b in range(4):
+            take(w_("lg3", 192, 240), w_(vn, pw * 3, pw * 3 + 320), tab("lx3", 3))
+            for b in (3, 0, 1, 2):
                 tt(w_("et3", b, 192, 4), w_(vn, pw * b, pw * b + 320), w_("lg3", 64 * b + 1, 64 * b + 49), ADD, tab("ux3", 3))
         quant(w_("ec%d" % t, 0, nq), w_("es%d" % t, 0, nq), w_("et%d" % t, 0, 4 * nq))
         send(t)
@@ -424,6 +419,9 @@ def rank_program(g, core, T, topo):
                 act(w_(fc, 640, 800), w_(vn, pw * 3 + 160, pw * 3 + 320))
 
         if t == 1:
+            ts(w_("pf", 8, 9), w_("pa", 1, 2), -1.0, MUL)
+            ts(w_("pf", 9, 10), w_("prow", 0, 1), -1.0, MUL)
+            ts(w_("pf", 10, 11), w_("prow", 0, 1), 1024.0, MUL, -15360.0, ADD)
             act(w_("ru1", 0, 176), w_("iow", 0, 320), tab("ux1", 11))
             late_masks()
             second_copies()
@@ -436,6 +434,11 @@ def rank_program(g, core, T, topo):
             for k in range(4):
                 scan(w_("sb1", 40 * k, 40 * k + 40), w_("rs8", 0, 40), w_("gb1", k, 160, 4))
                 scan(w_("st1", 40 * k, 40 * k + 40), w_("rs8", 0, 40), w_("gt1", 12 + k, 172, 4))
+            quant(w_("qv", 0, 128), w_("qvs", 0, 128), w_("vt", 0, 512))
+            for v in (w_("pp3", 0, 16), w_("px3", 0, 16), w_("lg3", 48, 256, 64), w_("cp", 0, 2), w_("cc2", 0, 80, 4), w_("eq3", 0, 16),
+                      w_("et2", 320, 512), w_("et3", 192, 512)):
+                fill(v, 0.0)
+            ts(w_("cp", 2, 3), w_("pf", 2, 3), 8.0, GE, 320.0, MUL)
             act(w_("pp2", 0, 40, 2), w_("sb1", 7, 160, 8))
             act(w_("pp2", 1, 40, 2), w_("st1", 7, 160, 8))
             act(w_("px2", 0, 40, 2), w_("st1", 7, 160, 8))
@@ -485,8 +488,6 @@ def rank_program(g, core, T, topo):
                 tt(w_("xt3", b, 1280, 4), w_(vn, pw * b, pw * b + 320), w_(fc, 320 * b, 320 * b + 320), ADD, w_("tab3", 0, 20))
             for b in (2, 3):
                 tt(w_("xt3", b, 1280, 4), w_("gg", 1280 + 320 * (b - 2), 1280 + 320 * (b - 1)), w_("pf%d" % b, 0, 320), ADD)
-        if t == 2:
-            quant(w_("qv", 0, 128), w_("qvs", 0, 128), w_("vt", 0, 512))
 
         for n in ("lc", "ls"):
             for k in (t, 0):

import numpy as np
from concourse.bass import DstId, RemoteDMATransfer
from concourse.mybir import dt, AluOpType, ActivationFunctionType

F32, BF, I32, U16, U8, Q8 = "float32", "bfloat16", "int32", "uint16", "uint8", "float8_e4m3fn_x4"
P = 128
NE = {1: 160, 2: 80, 3: 40}
NQ = {1: 160, 2: 128, 3: 128}
PW = {1: 480, 2: 400, 3: 320}
HL = {1: 4, 2: 2, 3: 1}
NZ = 88
LAND = {0: ("2", 40, NZ), 1: ("1", 0, 160), 2: ("2", 128, 80), 3: ("2", 0, 40)}
READ = {1: ("1", 0), 2: ("2", 80), 3: ("2", 0)}

SCRATCH = {}
ALIAS = {}


def _sb(name, n, d):
    SCRATCH[name] = ("sbuf", [P, n], d)


for _n, _c, _d in (
        ("xt0", 1280, BF), ("xt1", 1280, BF), ("xt2", 1280, BF), ("xt3", 2560, BF), ("ut", 512, BF), ("vt", 512, BF),
        ("twi", 20, I32), ("bt1", 20, U16), ("wcod", 512, Q8), ("wsca", 512, U8),
        ("qu", 128, Q8), ("qus", 128, U8), ("qu2", 128, Q8), ("qu2s", 128, U8), ("qv", 128, Q8), ("qvs", 128, U8),
        ("qe", 512, Q8), ("qes", 512, U8), ("qz", 128, Q8), ("qzs", 128, U8), ("zt", 512, BF),
        ("babs", 516, F32), ("bnd", 516, BF), ("pint", 1, I32), ("prow", 1, I32), ("pa", 4, I32), ("pf", 11, F32),
        ("uoi", 8, I32), ("uof", 8, U16), ("iow", 516, F32), ("rc8", 640, BF), ("rc4", 80, BF), ("upw", 640, F32),
        ("cc1", 640, BF), ("cs1", 640, BF), ("cc2", 80, BF), ("cs2", 80, BF),
        ("tabs", 128, U16), ("tab3", 32, U16), ("rb3", 64, F32), ("ru1", 176, F32), ("rb2", 96, F32),
        ("gg", 1920, BF), ("lg3", 256, BF), ("zt3", 192, BF), ("h3", 192, BF), ("z3", 192, BF), ("yo", 320, F32),
        ("ug1", 4 * 176, BF), ("ug2", 4 * 96, BF), ("qx", 1280, Q8), ("qxs", 1280, U8),
        ("rc_0", NZ, Q8), ("rs_0", NZ, U8), ("lc1", 160, Q8), ("ls1", 160, U8), ("lc2", 208, Q8), ("ls2", 208, U8)):
    _sb(_n, _c, _d)
_at = 0
for _n, _c in (
        ("t1", 320), ("t2", 224), ("t3", 160), ("t16", 320), ("m1", 320), ("m2", 224), ("m3", 160), ("m16", 320),
        ("dm2", 224), ("dm3", 160), ("dm16", 320), ("ones", 320), ("dp", 320),
        ("rs4", 40), ("rs8", 40), ("rs16", 48), ("cu1", 160), ("cu2", 80), ("cu3", 48), ("cp", 4),
        ("gp1", 320), ("sp1", 320), ("pp1", 160), ("pp2", 40), ("px2", 40), ("pp3", 16), ("px3", 16),
        ("gb1", 160), ("gt1", 176), ("sb1", 160), ("st1", 160), ("gb2", 96), ("gt2", 112), ("sb2", 96), ("st2", 96),
        ("eq1", 160), ("eq2", 40), ("eq3", 16), ("ma1", 160), ("mb1", 80), ("mc1", 40), ("rt1", 20),
        ("ma2", 40), ("mb2", 20), ("rt2", 10), ("mx2", 40), ("my2", 20), ("ry2", 10),
        ("ma3", 16), ("rt3", 8), ("mx3", 16), ("ry3", 8), ("tlf", 4), ("ucp", 4), ("us", 960),
        ("gs1", 320), ("gs2", 160), ("gs3", 96), ("sc1", 320), ("sc2", 160), ("sc3", 96)):
    ALIAS[_n] = ("fa", _at)
    _at += (_c + 7) // 8 * 8
_sb("fa", _at, F32)
for _t in (1, 2, 3):
    _sb("ss%d" % _t, 320, F32)
    _sb("v%d" % _t, 4 * PW[_t], BF)
    _sb("fc%d" % _t, 800, BF)
    _sb("et%d" % _t, 4 * NQ[_t], BF)
    _sb("ec%d" % _t, NQ[_t], Q8)
    _sb("es%d" % _t, NQ[_t], U8)
    _sb("rc_%d" % _t, NE[_t], Q8)
    _sb("rs_%d" % _t, NE[_t], U8)
for _b in range(4):
    SCRATCH["pf%d" % _b] = ("psum", [P, 512], F32)
    SCRATCH["ph%d" % _b] = ("psum", [P, 512], F32)

SEMAPHORES = ["kv", "ks", "kt", "kg", "lo", "hop0", "hop1", "hop2", "hop3", "ar0", "ar1", "ar2", "ar3",
              "dtw", "du", "dxa", "dxb", "dw", "dv", "dout"]

TB = {"ux1": 0, "lx1": 12, "uo1": 22, "up1": 32, "ux2": 52, "lx2": 60, "uo2": 66, "up2": 72, "tl2": 92, "bu2": 98,
      "lx3": 104, "ux3": 108, "uo3": 112, "tl3": 116, "bu3": 120}


def relays(T, topo, r):
    s, d = T.cores[r], T.cores[(r + 1) % len(T.cores)]
    c = [k for k in topo.cores_of(s) if k != s and T.rank_of(k) is None and topo.may_write(k, d)]
    c.sort(key=lambda k: (topo.die(k) != topo.die(s), k))
    return s, d, c[0], c[1]


def bits(es):
    return sum(1 << e for e in es)


def hand_on(g, core, T, topo):
    for r in range(len(T.cores)):
        s, d, ka, kb = relays(T, topo, r)
        if core not in (ka, kb):
            continue
        rid, pid = topo.addr(d, core)
        es = topo.engines(core, d)
        n_in = len(topo.engines(s, core))
        for t in (0, 1, 2, 3):
            b, a, n = LAND[t]
            g.wait_ge(T.sem["hop%d" % t], n_in)
            if core == ka:
                o, i = T["lc" + b][:, a:a + n].bitcast(dt.uint8), T["rc_%d" % t][:, 0:n].bitcast(dt.uint8)
            else:
                o, i = T["ls" + b][:, a:a + n], T["rs_%d" % t][:, 0:n]
            g.remote_dma(out_ap=o, in_ap=i, remote_sem=T.sem["ar%d" % t], local_sem=T.sem.lo, pid=pid, routing_id=rid, dma_engine_mask=bits(es))
        g.wait_ge(T.sem.lo, 4 * len(es))


def rank_program(g, core, T, topo):
    rank = T.rank_of(core)
    if rank is None:
        hand_on(g, core, T, topo)
        return
    A, AF = AluOpType, ActivationFunctionType
    ADD, MUL, EQ, GT, GE = A.add, A.mult, A.is_equal, A.is_gt, A.is_ge
    eng = {"v": g.vector, "s": g.scalar, "t": g.tensor, "y": g.sync, "g": g}
    cnt, known, clock = {}, {k: {} for k in eng}, {}
    wr, rd = {}, {}

    def w_(name, a, b, s=1):
        n, o = ALIAS.get(name, (name, 0))
        return (n, o + a, o + b, s)

    def ap(v):
        return T[v[0]][:, v[1]:v[2]:v[3]] if v[3] > 1 else T[v[0]][:, v[1]:v[2]]

    def clash(x, y):
        if x[1] >= y[2] or y[1] >= x[2]:
            return False
        return not (x[3] == y[3] and x[3] > 1 and (x[1] - y[1]) % x[3])

    def need(q, ev):
        s, n = ev
        if known[q].get(s, 0) >= n:
            return
        eng[q].wait_ge(T.sem[s], n)
        for k, m in clock.get(ev, {}).items():
            known[q][k] = max(known[q].get(k, 0), m)
        known[q][s] = max(known[q].get(s, 0), n)

    def order(q, reads, writes):
        evs = {}
        for v in reads:
            psum = SCRATCH[v[0]][0] == "psum"
            for x, ev, p in wr.get(v[0], []):
                if clash(v, x):
                    evs[ev[0]] = max(evs.get(ev[0], 0), ev[1])
            if psum:
                for x, ev, p in rd.get(v[0], []):
                    if p != q:
                        evs[ev[0]] = max(evs.get(ev[0], 0), ev[1])
        for v in writes:
            psum = SCRATCH[v[0]][0] == "psum"
            for x, ev, p in wr.get(v[0], []):
                if psum or clash(v, x):
                    evs[ev[0]] = max(evs.get(ev[0], 0), ev[1])
            for x, ev, p in rd.get(v[0], []):
                if (psum or clash(v, x)) and p != q:
                    evs[ev[0]] = max(evs.get(ev[0], 0), ev[1])
        for s in sorted(evs):
            need(q, (s, evs[s]))

    def emit(q, call, reads, writes, sem=None, inc=1):
        order(q, reads, writes)
        sem = sem or "k" + q
        cnt[sem] = cnt.get(sem, 0) + inc
        ev = (sem, cnt[sem])
        call().then_inc(T.sem[sem], inc)
        c = dict(known[q])
        c[sem] = cnt[sem]
        clock[ev] = c
        for v in writes:
            wr.setdefault(v[0], []).append((v, ev, q))
        for v in reads:
            rd.setdefault(v[0], []).append((v, ev, q))

    V, S, TE, G = g.vector, g.scalar, g.tensor, g

    def fill(v, c):
        emit("v", lambda: V.memset(ap(v), c), [], [v])

    def tt(o, a, b, op, off=None):
        if off is None:
            emit("v", lambda: V.tensor_tensor(ap(o), ap(a), ap(b), op), [a, b], [o])
        else:
            emit("v", lambda: V.tensor_tensor(ap(o), ap(a).indirect(ap(off)), ap(b), op), [a, b, off], [o])

    def ts(o, a, s1, op0, s2=None, op1=None):
        r = [a] + ([s1] if isinstance(s1, tuple) else [])
        s = ap(s1) if isinstance(s1, tuple) else s1
        if op1 is None:
            emit("v", lambda: V.tensor_scalar(ap(o), ap(a), s, None, op0), r, [o])
        else:
            emit("v", lambda: V.tensor_scalar(ap(o), ap(a), s, s2, op0, op1), r, [o])

    def cp(o, a):
        emit("v", lambda: V.tensor_copy(ap(o), ap(a)), [a], [o])

    def take(o, a, off):
        emit("v", lambda: V.tensor_copy(ap(o), ap(a).indirect(ap(off))), [a, off], [o])

    def put(o, off, a):
        emit("v", lambda: V.tensor_copy(ap(o).indirect(ap(off)), ap(a)), [a, off], [o])

    def scan(o, d0, d1):
        emit("v", lambda: V.tensor_tensor_scan(ap(o), ap(d0), ap(d1), 0.0, MUL, ADD), [d0, d1], [o])

    def quant(qo, so, i):
        emit("v", lambda: V.quantize_mx(ap(qo), ap(so), ap(i)), [i], [qo, so])

    def act(o, a, off=None, **kw):
        i = (lambda: ap(a).indirect(ap(off))) if off is not None else (lambda: ap(a))
        emit("s", lambda: S.activation(ap(o), i(), AF.Copy, **kw), [a] + ([off] if off is not None else []), [o])

    def mm(o, l, ls, m, ms):
        emit("t", lambda: TE.matmul_mx(ap(o), ap(l), ap(ls), ap(m), ap(ms), True, True), [l, ls, m, ms], [o])

    def iota(v, pattern, base=0, cm=0):
        if SCRATCH[v[0]][2] == I32:
            emit("g", lambda: G.iota(ap(v), pattern, base, cm), [], [v])
        else:
            emit("g", lambda: G.iota(ap(v), pattern, base, cm, allow_small_or_imprecise_dtypes=True), [], [v])

    def dma(q, o, i, reads, writes, sem):
        emit(q, lambda: eng[q].dma_start(o, i), reads, writes, sem, 16)

    def tab(name, k, j=0):
        return w_("tabs", TB[name] + j, TB[name] + j + k)

    def first_places():
        tt(w_("gp1", 0, 320), w_("iow", 0, 320), w_("m1", 0, 320), MUL, w_("bt1", 0, 20))
        yield 0
        for k in range(8):
            scan(w_("sp1", 40 * k, 40 * k + 40), w_("rs4", 0, 40), w_("gp1", k, 320, 8))
            yield k
        for l in range(2):
            act(w_("pp1", l, 160, 2), w_("sp1", 3, 320, 4))
        while True:
            yield 8
    gap = first_places()

    s_, d_, ka, kb = relays(T, topo, rank)
    lanes = [0]

    def send(t):
        n = LAND[t][2]
        c, s = ("ec%d" % t, "es%d" % t) if t else ("qz", "qzs")
        for k, o, i, r in ((ka, T["rc_%d" % t][:, 0:n].bitcast(dt.uint8), T[c][:, 0:n].bitcast(dt.uint8), w_(c, 0, n)),
                           (kb, T["rs_%d" % t][:, 0:n], T[s][:, 0:n], w_(s, 0, n))):
            order("g", [r], [])
            es = topo.engines(core, k)
            rid, pid = topo.addr(k, core)
            g.remote_dma(out_ap=o, in_ap=i, remote_sem=T.sem["hop%d" % t], local_sem=T.sem.lo, pid=pid, routing_id=rid, dma_engine_mask=bits(es))
            lanes[0] += len(es)

    dma("s", T.twi[:, :], T.tw[:, :], [], [w_("twi", 0, 20)], "dtw")
    dma("y", T.xt0[:, 0:640], T.x[:, 0:640], [], [w_("xt0", 0, 640)], "dxa")
    dma("s", T.ut[:, :], T.u[:, :], [], [w_("ut", 0, 512)], "du")
    dma("y", T.xt0[:, 640:1280], T.x[:, 640:1280], [], [w_("xt0", 640, 1280)], "dxb")
    need("y", ("dxb", 16))
    dma("y", T.wcod[:, 0:512].bitcast(dt.uint8), T.wc[:, :], [], [w_("wcod", 0, 512)], "dw")
    dma("y", T.wsca[:, 0:512], T.ws[:, :], [], [w_("wsca", 0, 512)], "dw")
    for n in ("wcod", "wsca"):
        wr[n] = [(w_(n, 0, 512), ("dw", 32), "y")]
    dma("y", T.vt[:, :], T.v[:, :], [], [w_("vt", 0, 512)], "dv")

    fill(w_("zt", 0, 512), 0.0)
    fill(w_("ones", 0, 80), 1.0)
    quant(w_("qz", 0, 128), w_("qzs", 0, 128), w_("zt", 0, 512))
    iota(w_("pint", 0, 1), [[1, 1]], 0, 1)
    iota(w_("t1", 0, 320), [[0, 10], [1, 4], [0, 8]])
    iota(w_("uoi", 0, 8), [[16, 8]])
    iota(w_("iow", 0, 516), [[1, 516]])
    send(0)
    for n, m, k in (("rs8", 40, 8), ("rs16", 48, 16), ("rc4", 80, 4)):
        o, i = w_(n, 0, m), w_("ones", 0, m)
        emit("g", lambda: G.affine_select(ap(o), ap(i), [[0, m // k], [1, k]], GT, 0.0, 0, 0), [i], [o])
    iota(w_("t16", 0, 320), [[0, 20], [1, 16]])
    iota(w_("t2", 0, 224), [[0, 7], [1, 8], [0, 4]])
    iota(w_("t3", 0, 160), [[0, 5], [1, 16], [0, 2]])
    iota(w_("cu1", 0, 156), [[1, 156]], 324)
    iota(w_("cu1", 156, 160), [[1, 4]], 320)
    iota(w_("cu2", 0, 78), [[1, 78]], 322)
    iota(w_("cu2", 78, 80), [[1, 2]], 320)
    iota(w_("cu3", 0, 39), [[1, 39]], 321)
    iota(w_("cu3", 39, 48), [[1, 9]], 320)

    fill(w_("rs4", 0, 40), 1.0)
    fill(w_("cc1", 0, 640, 8), 0.0)
    ts(w_("pf", 7, 8), w_("pint", 0, 1), -4.0, MUL, -3.0, ADD)
    ts(w_("prow", 0, 1), w_("pint", 0, 1), 15, A.bitwise_and)
    fill(w_("rc8", 0, 640), 1.0)
    ts(w_("pa", 0, 1), w_("prow", 0, 1), 2, A.arith_shift_right)
    ts(w_("pa", 1, 2), w_("prow", 0, 1), 1, A.arith_shift_right)
    ts(w_("pa", 2, 3), w_("prow", 0, 1), 3, A.bitwise_and)
    ts(w_("pa", 3, 4), w_("prow", 0, 1), 1, A.bitwise_and)
    cp(w_("pf", 2, 3), w_("prow", 0, 1))
    cp(w_("pf", 0, 2), w_("pa", 0, 2))
    cp(w_("pf", 3, 5), w_("pa", 2, 4))
    ts(w_("pf", 5, 6), w_("pa", 2, 3), 4.0, ADD)
    ts(w_("pf", 6, 7), w_("pa", 3, 4), 2.0, ADD)
    fill(w_("rs4", 0, 40, 4), 0.0)
    fill(w_("rc8", 0, 640, 8), 0.0)
    emit("s", lambda: S.activation(T.babs[:, 0:516], T.iow[:, 0:516], AF.Abs, bias=T.pf[:, 7:8]), [w_("iow", 0, 516), w_("pf", 7, 8)], [w_("babs", 0, 516)])
    emit("s", lambda: S.activation(T.bnd[:, 0:516], T.babs[:, 0:516], AF.Relu, bias=0.5, scale=-0.5), [w_("babs", 0, 516)], [w_("bnd", 0, 516)])
    ts(w_("m1", 0, 320), w_("t1", 0, 320), w_("pf", 0, 1), EQ)
    cp(w_("uof", 0, 8), w_("uoi", 0, 8))
    cp(w_("bt1", 0, 20), w_("twi", 0, 20))
    next(gap)
    quant(w_("qu", 0, 128), w_("qus", 0, 128), w_("ut", 0, 512))
    quant(w_("qx", 0, 160), w_("qxs", 0, 160), w_("xt0", 0, 640))
    emit("v", lambda: V.tensor_copy(T.qu2[:, 0:128].bitcast(dt.uint32), T.qu[:, 0:128].bitcast(dt.uint32).indirect(T.uof[:, 0:8])),
         [w_("qu", 0, 128), w_("uof", 0, 8)], [w_("qu2", 0, 128)])
    act(w_("qu2s", 0, 128), w_("qus", 0, 128), w_("uof", 0, 8))

    def late_masks():
        for m, t, n, c in (("m16", "t16", 320, 9), ("m2", "t2", 224, 8), ("m3", "t3", 160, 9)):
            i, o, d, b = w_(t, 0, n), w_(m, 0, n), w_("d" + m, 0, n), w_("pf", c, c + 1)
            emit("s", lambda: S.activation(ap(d), ap(i), AF.Abs, bias=ap(b)), [i, b], [d])
            emit("s", lambda: S.activation(ap(o), ap(d), AF.Relu, bias=1.0, scale=-1.0), [d], [o])
            if m == "m16":
                act(w_("dp", 0, 320), o, scale=-1000000.0, bias=1024.0)

    def place_list(t, out, clip):
        u = 320 * (t - 1)
        o, a, b, e = w_("us", u, u + 320), w_("dp", 0, 320), w_("upw", 0, 320), w_("us", u + 15, u + 320, 16)
        emit("v", lambda: V.tensor_tensor_scan(ap(o), ap(a), ap(b), 0.0, ADD, A.max), [a, b], [o])
        if clip:
            ts(out, e, w_("pf", 10, 11), ADD, 319.0, A.min)
        else:
            ts(out, e, w_("pf", 10, 11), ADD)

    for t in (1, 2, 3):
        h = HL[t]
        w = 2 * h
        ne, nq, pw = NE[t], NQ[t], PW[t]
        qo = 320 * (t - 1)
        x = "xt%d" % (t - 1)
        for i in range(2):
            if (t, i) != (1, 0):
                quant(w_("qx", qo + 160 * i, qo + 160 * i + 160), w_("qxs", qo + 160 * i, qo + 160 * i + 160), w_(x, 640 * i, 640 * i + 640))
            mm(w_("ph%d" % i, 0, 160), w_("qu2", 0, 128), w_("qu2s", 0, 128), w_("qx", qo + 160 * i, qo + 160 * i + 160), w_("qxs", qo + 160 * i, qo + 160 * i + 160))
        if t == 1:
            for b in (3, 0, 1, 2):
                quant(w_("qe", 128 * b, 128 * b + 128), w_("qes", 128 * b, 128 * b + 128), w_("bnd", 3 - b, 515 - b))
        for b in (3, 0, 1, 2):
            mm(w_("pf%d" % b, 0, 320), w_("qe", 128 * b, 128 * b + 128), w_("qes", 128 * b, 128 * b + 128), w_("qx", qo, qo + 320), w_("qxs", qo, qo + 320))
        ss, gs, sc, vn = "ss%d" % t, "gs%d" % t, "sc%d" % t, "v%d" % t
        act(w_(ss, 0, 160), w_("ph0", 0, 160))
        cp(w_(ss, 160, 320), w_("ph1", 0, 160))
        for b in ((3, 0, 1, 2) if t > 1 else (3, 0)):
            act(w_(vn, pw * b, pw * b + 320), w_("pf%d" % b, 0, 320))
        if t == 1:
            next(gap)
        ng = 40 * w if t < 3 else 96
        bt = w_("bt1", 0, 20) if t == 1 else tab("lx%d" % (t - 1), ng // 16)
        tt(w_(gs, 0, ng), w_(ss, 0, 320), w_("m%d" % t, 0, ng), MUL, bt)
        if t == 1:
            next(gap)
            next(gap)
        L = 40 if t < 3 else 48
        T_ = 16 // h
        rsn = {1: "rs4", 2: "rs8", 3: "rs16"}[t]
        for k in range(w):
            scan(w_(sc, L * k, L * k + L), w_(rsn, 0, L), w_(gs, k, ng, w))
        if t == 1:
            next(gap)
            next(gap)
        nc = L // T_
        sv = lambda k0, k1: w_(sc, L * k0 + T_ - 1, L * k1, T_)
        if t < 3:
            cc, cs, eq, rt = "cc%d" % t, "cs%d" % t, "eq%d" % t, "rt%d" % t
            for d in range(1, w):
                above, below = w_(cc, d, w * nc * (w - d), w), w_(cc, w * nc * d + w - d, w * nc * w, w)
                tt(above, sv(d, w), sv(0, w - d), GT)
                if t == 1:
                    act(below, above, scale=-1.0, bias=1.0)
                else:
                    tt(below, sv(0, w - d), sv(d, w), GE)
            if t == 1:
                while next(gap) < 8:
                    pass
                for b in (1, 2):
                    act(w_(vn, pw * b, pw * b + 320), w_("pf%d" % b, 0, 320))
            scan(w_(cs, 0, w * w * nc), w_("rc8" if t == 1 else "rc4", 0, w * w * nc), w_(cc, 0, w * w * nc))
            n2 = 2 * w * nc
            ts(w_(eq, 0, n2, 2), w_(cs, w - 1, w * w * nc, w), w_("pf", 2 + t, 3 + t), EQ)
            ts(w_(eq, 1, n2, 2), w_(cs, w - 1, w * w * nc, w), w_("pf", 4 + t, 5 + t), EQ)

            def pick(names, pay):
                tt(w_(names[0], 0, n2), w_(eq, 0, n2), w_(pay, 0, n2), MUL)
                n = n2 // 2
                for a, o in zip(names, names[1:]):
                    tt(w_(o, 0, n), w_(a, 0, n), w_(a, n, 2 * n), ADD)
                    n //= 2
            pick(("ma1", "mb1", "mc1", "rt1") if t == 1 else ("ma2", "mb2", "rt2"), "pp%d" % t)
            nu = 16 + ne
            cp(tab("ux%d" % t, nc, 1), w_(rt, 1, 2 * nc, 2))
            cp(tab("ux%d" % t, 1), w_(rt, 2 * nc - 1, 2 * nc))
            cp(tab("lx%d" % t, nc), w_(rt, 0, 2 * nc, 2))
            ug = "ug%d" % t
            for b in (0, 1, 2):
                act(w_(ug, nu * b, nu * b + nu), w_(vn, pw * b, pw * b + 320), tab("ux%d" % t, nu // 16))
            take(w_(ug, nu * 3, nu * 4), w_(vn, pw * 3, pw * 3 + 320), tab("ux%d" % t, nu // 16))
            for b in (3, 0, 1, 2):
                tt(w_("et%d" % t, b, 4 * ne, 4), w_(vn, pw * b, pw * b + 320), w_(ug, nu * b + 16 - h, nu * b + 16 - h + ne), ADD, tab("lx%d" % t, ne // 16))
        else:
            for o, f in ((0, GE), (4, GT), (8, GT), (12, GE)):
                a, b = (sv(0, 1), sv(1, 2)) if f == GE else (sv(1, 2), sv(0, 1))
                tt(w_("eq3", o, o + 3), a, b, f)
            tt(w_("ma3", 0, 16), w_("eq3", 0, 16), w_("pp3", 0, 16), MUL)
            tt(w_("rt3", 0, 8), w_("ma3", 0, 8), w_("ma3", 8, 16), ADD)
            cp(tab("lx3", 8), w_("rt3", 0, 8))
            for b in (0, 1, 2):
                act(w_("lg3", 64 * b, 64 * b + 48), w_(vn, pw * b, pw * b + 320), tab("lx3", 3))
            take(w_("lg3", 192, 240), w_(vn, pw * 3, pw * 3 + 320), tab("lx3", 3))
            for b in (3, 0, 1, 2):
                tt(w_("et3", b, 192, 4), w_(vn, pw * b, pw * b + 320), w_("lg3", 64 * b + 1, 64 * b + 49), ADD, tab("ux3", 3))
        quant(w_("ec%d" % t, 0, nq), w_("es%d" % t, 0, nq), w_("et%d" % t, 0, 4 * nq))
        send(t)

        fc = "fc%d" % t

        def second_copies():
            for b in (0, 1):
                act(w_(fc, 320 * b, 320 * b + 320), w_(vn, pw * b, pw * b + 320))
            if t < 3:
                act(w_(fc, 640, 800), w_(vn, pw * 3 + 160, pw * 3 + 320))

        if t == 1:
            ts(w_("pf", 8, 9), w_("pa", 1, 2), -1.0, MUL)
            ts(w_("pf", 9, 10), w_("prow", 0, 1), -1.0, MUL)
            ts(w_("pf", 10, 11), w_("prow", 0, 1), 1024.0, MUL, -15360.0, ADD)
            act(w_("ru1", 0, 176), w_("iow", 0, 320), tab("ux1", 11))
            late_masks()
            second_copies()
            cp(tab("uo1", 10), w_("rt1", 1, 20, 2))
            put(w_("upw", 0, 640), tab("uo1", 10), w_("cu1", 0, 160))
            put(w_("upw", 0, 640), tab("lx1", 10), w_("ru1", 12, 172))
            place_list(1, tab("up1", 20), False)
            tt(w_("gb1", 0, 160), w_("iow", 0, 320), w_("m2", 0, 160), MUL, tab("lx1", 10))
            tt(w_("gt1", 0, 176), w_("iow", 0, 320), w_("m2", 20, 196), MUL, tab("ux1", 11))
            for k in range(4):
                scan(w_("sb1", 40 * k, 40 * k + 40), w_("rs8", 0, 40), w_("gb1", k, 160, 4))
                scan(w_("st1", 40 * k, 40 * k + 40), w_("rs8", 0, 40), w_("gt1", 12 + k, 172, 4))
            quant(w_("qv", 0, 128), w_("qvs", 0, 128), w_("vt", 0, 512))
            for v in (w_("pp3", 0, 16), w_("px3", 0, 16), w_("lg3", 48, 256, 64), w_("cp", 0, 2), w_("cc2", 0, 80, 4), w_("eq3", 0, 16),
                      w_("et2", 320, 512), w_("et3", 192, 512)):
                fill(v, 0.0)
            ts(w_("cp", 2, 3), w_("pf", 2, 3), 8.0, GE, 320.0, MUL)
            act(w_("pp2", 0, 40, 2), w_("sb1", 7, 160, 8))
            act(w_("pp2", 1, 40, 2), w_("st1", 7, 160, 8))
            act(w_("px2", 0, 40, 2), w_("st1", 7, 160, 8))
            act(w_("px2", 1, 40, 2), w_("sb1", 7, 160, 8))
        elif t == 2:
            pick(("mx2", "my2", "ry2"), "px2")
            cp(tab("bu2", 5, 1), w_("ry2", 1, 10, 2))
            cp(tab("bu2", 1), w_("ry2", 9, 10))
            act(w_("rb2", 0, 96), w_("iow", 0, 320), tab("bu2", 6))
            second_copies()
            cp(tab("tl2", 5), w_("ry2", 0, 10, 2))
            cp(tab("uo2", 5), w_("rt2", 1, 10, 2))
            put(w_("upw", 0, 640), tab("uo2", 5), w_("cu2", 0, 80))
            put(w_("upw", 0, 640), tab("tl2", 5), w_("rb2", 14, 94))
            place_list(2, tab("up2", 20), False)
            cp(tab("lx2", 1, 5), w_("rt2", 0, 1))
            cp(tab("ux2", 1, 6), w_("rt2", 1, 2))
            tt(w_("gb2", 0, 96), w_("iow", 0, 320), w_("m3", 0, 96), MUL, tab("lx2", 6))
            tt(w_("gt2", 0, 112), w_("iow", 0, 320), w_("m3", 18, 130), MUL, tab("ux2", 7))
            for k in range(2):
                scan(w_("sb2", 48 * k, 48 * k + 48), w_("rs16", 0, 48), w_("gb2", k, 96, 2))
                scan(w_("st2", 48 * k, 48 * k + 48), w_("rs16", 0, 48), w_("gt2", 14 + k, 110, 2))
            for k in range(2):
                for o, s in ((0, "sb2"), (4, "st2")):
                    act(w_("pp3", 8 * k + o, 8 * k + o + 3), w_(s, 48 * k + 15, 48 * k + 48, 16))
                    act(w_("px3", 8 * k + 4 - o, 8 * k + 7 - o), w_(s, 48 * k + 15, 48 * k + 48, 16))
        else:
            tt(w_("mx3", 0, 16), w_("eq3", 0, 16), w_("px3", 0, 16), MUL)
            tt(w_("ry3", 0, 8), w_("mx3", 0, 8), w_("mx3", 8, 16), ADD)
            cp(tab("bu3", 3), w_("ry3", 4, 7))
            act(w_("rb3", 1, 49), w_("iow", 0, 320), tab("bu3", 3))
            act(w_("rb3", 0, 1), w_("rb3", 40, 41))
            second_copies()
            tt(w_("tlf", 0, 3), w_("ry3", 0, 3), w_("cp", 0, 3), ADD)
            tt(w_("ucp", 0, 3), w_("rt3", 4, 7), w_("cp", 0, 3), ADD)
            cp(tab("tl3", 3), w_("tlf", 0, 3))
            for b in range(4):
                ts(w_("tab3", 20 + 3 * b, 23 + 3 * b), w_("ucp", 0, 3), 4.0, MUL, float(b), ADD)
            cp(tab("uo3", 3), w_("ucp", 0, 3))
            put(w_("upw", 0, 640), tab("tl3", 3), w_("rb3", 0, 48))
            place_list(3, w_("tab3", 0, 20), True)
            for b in range(4):
                act(w_("zt3", 48 * b, 48 * b + 48), w_(vn, pw * b, pw * b + 320), tab("ux3", 3))
            for b in (2, 3):
                act(w_("gg", 1280 + 320 * (b - 2), 1280 + 320 * (b - 1)), w_(vn, pw * b, pw * b + 320), w_("tab3", 0, 20))
            for b in (0, 1):
                tt(w_("xt3", b, 1280, 4), w_(vn, pw * b, pw * b + 320), w_(fc, 320 * b, 320 * b + 320), ADD, w_("tab3", 0, 20))
            for b in (2, 3):
                tt(w_("xt3", b, 1280, 4), w_("gg", 1280 + 320 * (b - 2), 1280 + 320 * (b - 1)), w_("pf%d" % b, 0, 320), ADD)

        for n in ("lc", "ls"):
            for k in (t, 0):
                b, a, m = LAND[k]
                wr.setdefault(n + b, []).append((w_(n + b, a, a + m), ("ar%d" % k, 2 * len(topo.engines(ka, d_))), "r"))
        rb, ra = READ[t]
        hs = LAND[t][1] - ra
        for b in ((0, 2, 1, 3) if t < 3 else (0, 1, 2, 3)):
            mm(w_("ph%d" % b, 0, nq), w_("wcod", 128 * b, 128 * b + 128), w_("wsca", 128 * b, 128 * b + 128), w_("lc" + rb, ra, ra + nq), w_("ls" + rb, ra, ra + nq))
        half = 0.015625
        if t < 3:
            gq = 640 * (t - 1)
            win = lambda b: w_(vn, pw * b, pw * b + pw)
            hv = lambda b: w_(vn, pw * b + 320, pw * b + 320 + ne)
            hp = lambda b: w_("ph%d" % b, hs, hs + ne)
            ob, up = "xt%d" % t, "up%d" % t
            act(hv(2), hp(2), scale=half)
            act(hv(1), hp(1), scale=half)
            act(w_("gg", gq, gq + 320), win(2), tab(up, 20))
            act(hv(3), hp(3), scale=half)
            act(w_("gg", gq + 320, gq + 480), win(3), tab(up, 10))
            ts(hv(0), hp(0), half, MUL)
            for b in (0, 1):
                tt(w_(ob, b, 1280, 4), win(b), w_(fc, 320 * b, 320 * b + 320), ADD, tab(up, 20))
            tt(w_(ob, 640 + 3, 1280, 4), win(3), w_(fc, 640, 800), ADD, tab(up, 10, 10))
            tt(w_(ob, 2, 1280, 4), w_("gg", gq, gq + 320), w_("pf2", 0, 320), ADD)
            tt(w_(ob, 3, 640, 4), w_("gg", gq + 320, gq + 480), w_("pf3", 0, 160), ADD)
        else:
            for b in range(4):
                act(w_("h3", 48 * b, 48 * b + 48), w_("ph%d" % b, 0, 48), scale=half)
            for b in range(4):
                tt(w_("z3", 48 * b, 48 * b + 48), w_("zt3", 48 * b, 48 * b + 48), w_("h3", 48 * b, 48 * b + 48), ADD)
                if b % 2:
                    put(w_("xt3", 0, 2560), w_("tab3", 14 + 6 * (b // 2 + 1), 20 + 6 * (b // 2 + 1)), w_("z3", 96 * (b // 2), 96 * (b // 2) + 96))

    for i in range(2):
        a = 960 + 160 * i
        quant(w_("qx", a, a + 160), w_("qxs", a, a + 160), w_("xt3", 640 * i, 640 * i + 640))
        mm(w_("ph%d" % i, 0, 160), w_("qv", 0, 128), w_("qvs", 0, 128), w_("qx", a, a + 160), w_("qxs", a, a + 160))
    put(w_("upw", 0, 640), tab("uo3", 3), w_("cu3", 0, 48))
    dma("y", T.oc[:, :], T.qx[:, 960:1280].bitcast(dt.uint8), [w_("qx", 960, 1280)], [], "dout")
    for k in range(4):
        dma("y", T.osc[4 * k:4 * k + 4, 0:320], T.qxs[32 * k:32 * k + 4, 960:1280], [w_("qxs", 960, 1280)], [], "dout")
    dma("y", T.op[:, :], T.upw[0:128:16, 0:320], [w_("upw", 0, 320)], [], "dout")
    act(w_("yo", 0, 160), w_("ph0", 0, 160))
    cp(w_("yo", 160, 320), w_("ph1", 0, 160))
    dma("s", T.y[:, 0:160], T.yo[:, 0:160], [w_("yo", 0, 160)], [], "dout")
    dma("y", T.y[:, 160:320], T.yo[:, 160:320], [w_("yo", 160, 320)], [], "dout")
    g.wait_ge(T.sem.lo, lanes[0])
    for s in sorted(cnt):
        g.wait_ge(T.sem[s], cnt[s])
    for t in (0, 1, 2, 3):
        g.wait_ge(T.sem["ar%d" % t], 2 * len(topo.engines(ka, d_)))
